import numpy as np
import ml_dtypes


def mxq(x, axis, fmt="e4m3"):
    dtype, down = {"e4m3": (ml_dtypes.float8_e4m3fn, 7), "e5m2": (ml_dtypes.float8_e5m2, 14)}[fmt]
    v = np.moveaxis(np.asarray(x, np.float32).astype(ml_dtypes.bfloat16).astype(np.float64), axis, -1)
    blocks = v.reshape(v.shape[:-1] + (-1, 32))
    amax = np.abs(blocks).max(-1, keepdims=True)
    byte = np.maximum(np.where(amax > 0, np.frexp(amax)[1] - 1 + 127, 0) - down, 1)
    scale = np.exp2(byte - 127.0)
    codes = (blocks / scale).astype(np.float32).astype(dtype).astype(np.float64)
    return np.moveaxis((codes * scale).reshape(v.shape), -1, axis)


WIDE = False


def mx_kscale(k):
    if not WIDE:
        return np.ones(k)
    levels = np.array([10, -10, 5, -5, 0])
    if k % 512:
        return np.exp2(np.random.permutation(np.resize(levels, k // 32))).repeat(32)
    a = np.empty((k // 512, 16))
    for p in range(k // 512):
        a[p, :8] = np.random.permutation(np.resize(levels, 8))
        for g in range(8):
            far = levels[np.abs(levels - a[p, g]) >= 10]
            a[p, g + 8] = far[np.random.randint(len(far))]
    return np.exp2(a.ravel()).repeat(32)


def f64(x):
    return np.asarray(x).astype(np.float64)


def striped(idx):
    return np.tile(idx.reshape(-1, 16).T, (8, 1)).astype(np.uint16)


def unstriped(offs):
    return offs[:16].T.reshape(-1).astype(np.int64)


def pack_weight(w):
    k, n = w.shape
    w = f64(np.asarray(w, np.float32).astype(ml_dtypes.bfloat16)).reshape(k // 32, 32, n)
    amax = np.abs(w).max(1)
    byte = np.clip(np.where(amax > 0, np.frexp(amax)[1] - 1 + 127 - 7, 1), 1, 254)
    scaled = (w * np.exp2(127.0 - byte)[:, None, :]).reshape(k, n).astype(np.float32)
    words = np.ascontiguousarray(scaled.reshape(k // 512, 128, 4, n).transpose(0, 1, 3, 2)).astype(ml_dtypes.float8_e4m3fn).view(np.uint8)
    return words, np.ascontiguousarray(byte.astype(np.uint8).reshape(k // 512, 16, n))


def unpack_weight(words, scales):
    g, p, n, _ = words.shape
    vals = np.ascontiguousarray(words).view(ml_dtypes.float8_e4m3fn).astype(np.float64) * np.repeat(np.exp2(scales.astype(np.float64) - 127.0), 8, axis=1)[..., None]
    return vals.transpose(0, 1, 3, 2).reshape(g * 512, n)


def planes(y):
    n, m = y.shape
    v = y.astype(np.float32).astype(ml_dtypes.bfloat16).astype(np.float64).reshape(n // 32, 32, m)
    top = np.abs(v).max(1)
    byte = np.clip(np.where(top > 0, np.frexp(top)[1] - 1 + 127 - 7, 1), 1, 254)
    codes = (v * np.exp2(127.0 - byte)[:, None, :]).reshape(n, m).astype(np.float32).astype(ml_dtypes.float8_e4m3fn).view(np.uint8)
    words = codes.reshape(n // 512, 128, 4, m).transpose(0, 1, 3, 2)
    return np.ascontiguousarray(words), np.ascontiguousarray(byte.astype(np.uint8).reshape(n // 512, 16, m))


def gelu(v):
    return 0.5 * v * (1.0 + np.tanh(np.sqrt(2.0 / np.pi) * (v + 0.044715 * v**3)))


K, T, S, D, N = 512, 2048, 1024, 3, 512
P = 2 ** 7


def setup_inputs():
    n = np.random.standard_normal
    s = mx_kscale(K)[:, None]
    packed_xT = pack_weight(n((K, T)) * s)
    return {
        "x_words": packed_xT[0],
        "x_scales": packed_xT[1],
        "w1": (n((K, N)) / np.sqrt(K) / s).astype(np.float32),
        "w2": (n((K, N)) / np.sqrt(K) / s).astype(np.float32),
        "w3": (n((K, N)) / np.sqrt(K) / s).astype(np.float32),
        "gate": (np.tile(np.random.dirichlet(np.ones(D), T).T[:, None, :], (1, P, 1))).astype(np.float32),
        "offs": striped(np.random.permutation(T)[:S]),
    }


def reference(x_words, x_scales, w1, w2, w3, gate, offs):
    xq = unpack_weight(x_words, x_scales)[:, unstriped(offs)]
    g0 = f64(gate)[0, :1][:, unstriped(offs)]
    g1 = f64(gate)[1, :1][:, unstriped(offs)]
    g2 = f64(gate)[2, :1][:, unstriped(offs)]
    out_0 = (gelu(mxq(f64(w1), 0, "e4m3").T @ xq)) * g0 + (gelu(mxq(f64(w2), 0, "e4m3").T @ xq)) * g1 + (gelu(mxq(f64(w3), 0, "e4m3").T @ xq)) * g2
    return (out_0,) + planes(out_0)

@@ -1,0 +1,197 @@
+from contextlib import ExitStack
+
+import concourse.mybir as mybir
+from concourse.masks import make_identity
+
+K, T, S, D, N = 512, 2048, 1024, 3, 512
+FLOPS = 2 * D * K * N * S
+BYTES = K * T + 16 * T + D * K * N * 4 + D * T * 4 + 128 * (S // 16) * 2 + N * S * 4 + N * S + 16 * S
+
+F32 = mybir.dt.float32
+BF16 = mybir.dt.bfloat16
+I32 = mybir.dt.int32
+U32 = mybir.dt.uint32
+U16 = mybir.dt.uint16
+U8 = mybir.dt.uint8
+FP8X4 = mybir.dt.float8_e4m3fn_x4
+GELU = mybir.ActivationFunctionType.Gelu_apprx_tanh
+MULT = mybir.AluOpType.mult
+
+P = 128
+PACK = 4
+TILES = S // P
+HALF = N // 2
+GATE_STEP = 4
+WORD_PIECE = 256
+
+
+def interleave(copy, dst, src):
+    copy(
+        out=dst.rearrange("p (c i t) -> p c t i", i=4, t=PACK),
+        in_=src.rearrange("p t (c i) -> p c t i", i=4),
+    )
+
+
+def tile_picked_zsmoe_gelu_po_kernel(tc, x_words, x_scales, w1, w2, w3, gate, offs, out_0, out_1, out_2):
+    nc = tc.nc
+    weights = (w1, w2, w3)
+    with ExitStack() as ctx:
+        keep = ctx.enter_context(tc.tile_pool(name="keep", bufs=1))
+        psum = ctx.enter_context(tc.psum_pool(name="psum", bufs=4))
+
+        offsets = keep.tile([P, S // 16], U16, name="offsets")
+        word_win = keep.tile([P, T], U32, name="word_win", align_bytes=64)
+        scale_win = keep.tile([P, T], U8, name="scale_win", align_bytes=64)
+        gate_win = keep.tile([P, T], F32, name="gate_win", align_bytes=64)
+        ident = keep.tile([P, P], F32, name="ident", align_bytes=64)
+        warm = keep.tile([P, 2], F32, name="warm")
+
+        nc.vector.memset(warm[:, 0:1], 0.0)
+        nc.vector.memset(scale_win[:].bitcast(I32), 0)
+        nc.vector.memset(gate_win[:], 0.0)
+        make_identity(nc, ident[:])
+
+        nc.sync.dma_start(offsets[:], offs)
+        w_raw = {}
+
+        def load_w1(h):
+            w_raw[0, h] = keep.tile([P, PACK, HALF], F32, name=f"w_raw0{h}", align_bytes=64)
+            nc.sync.dma_start(w_raw[0, h][:], w1[:, h * HALF:(h + 1) * HALF].rearrange("(p t) m -> p t m", t=PACK))
+
+        load_w1(0)
+        for q in range(4):
+            nc.sync.dma_start(scale_win[32 * q:32 * q + 4, :].bitcast(I32), x_scales[0, 4 * q:4 * q + 4, :].bitcast(I32))
+        load_w1(1)
+        nc.sync.dma_start(word_win[:].bitcast(I32), x_words[0].rearrange("p n t -> p (n t)").bitcast(I32))
+        for d in (1, 2):
+            w_raw[d] = keep.tile([P, PACK, N], F32, name=f"w_raw{d}", align_bytes=64)
+            nc.sync.dma_start(w_raw[d][:], weights[d].rearrange("(p t) m -> p t m", t=PACK))
+        nc.sync.dma_start(gate_win[GATE_STEP:GATE_STEP * (D + 1):GATE_STEP, :], gate[:, 0, :])
+
+        nc.scalar.activation(warm[:, 1:2], warm[:, 0:1], GELU)
+
+        w_bf = [keep.tile([P, PACK * N], BF16, name=f"w_bf{d}", align_bytes=64) for d in range(D)]
+        w_codes = [keep.tile([P, N], U32, name=f"w_codes{d}", align_bytes=64) for d in range(D)]
+        w_scales = [keep.tile([P, N], U8, name=f"w_scales{d}", align_bytes=64) for d in range(D)]
+
+        def quantize_w(d, cols):
+            nc.vector.quantize_mx(
+                out=w_codes[d][:, cols].bitcast(FP8X4),
+                scales=w_scales[d][:, cols],
+                in_=w_bf[d][:, PACK * cols.start:PACK * cols.stop],
+            )
+
+        for h in range(2):
+            interleave(nc.scalar.copy, w_bf[0][:, h * PACK * HALF:(h + 1) * PACK * HALF], w_raw[0, h][:])
+
+        gate_rows = keep.tile([P, S], F32, name="gate_rows", align_bytes=64)
+
+        tok_scales = [keep.tile([P, S // 2], U8, name=f"tok_scales{u}", align_bytes=64) for u in range(2)]
+        tok_words = [keep.tile([P, WORD_PIECE], U32, name=f"tok_words{u}", align_bytes=64) for u in range(S // WORD_PIECE)]
+
+        def gather_scales(u):
+            nc.vector.tensor_copy(tok_scales[u][:], scale_win[:].indirect(offsets[:, 32 * u:32 * (u + 1)]))
+
+        def gather_words(u):
+            nc.vector.tensor_copy(tok_words[u][:], word_win[:].indirect(offsets[:, 16 * u:16 * (u + 1)]))
+
+        gate_cols = keep.tile([P, TILES, D], F32, name="gate_cols")
+
+        def turn_gates(u):
+            bank = psum.tile([P, PACK, P], F32, name="turned", tag="turned")
+            for a in range(4):
+                i = 4 * u + a
+                nc.tensor.transpose(bank[:, a, :], gate_rows[:, i * P:(i + 1) * P], ident[:])
+            nc.vector.tensor_copy(gate_cols[:, 4 * u:4 * u + 4, :], bank[:, :, GATE_STEP:GATE_STEP * (D + 1):GATE_STEP])
+
+        def gather_gates(u):
+            nc.vector.tensor_copy(gate_rows[:, u * (S // 2):(u + 1) * (S // 2)], gate_win[:].indirect(offsets[:, 32 * u:32 * (u + 1)]))
+
+        gather_scales(0)
+        gather_scales(1)
+        quantize_w(0, slice(0, HALF))
+        quantize_w(0, slice(HALF, N))
+        for u in range(S // WORD_PIECE):
+            gather_words(u)
+        for d in (1, 2):
+            interleave(nc.vector.tensor_copy, w_bf[d][:], w_raw[d][:])
+            quantize_w(d, slice(0, N))
+        gather_gates(0)
+        gather_gates(1)
+
+        y_codes = keep.tile([P, S], U32, name="y_codes", align_bytes=64)
+        y_scales = keep.tile([P, S], U8, name="y_scales", align_bytes=64)
+        out_rows = out_0.rearrange("(p t) j -> p t j", t=PACK)
+        out_words = out_1[0].rearrange("p n t -> p (n t)").bitcast(I32)
+
+        half = TILES // 2
+        accs = [psum.tile([P, N], F32, name=f"acc{b}", tag=f"acc{b}", bufs=1) for b in range(4)]
+        units = [(i, 0) for i in range(TILES)] + [(i, d) for d in (1, 2) for i in range(half)]
+        units = units + [(i, d) for i in range(half, TILES) for d in (1, 2)]
+        groups = [(0, 1), (2, 3), (4, 5), (6,), (7,)]
+
+        acts = {}
+        scaled = {}
+        turned = {}
+        ys = {}
+
+        def product(n):
+            i, d = units[n]
+            acc = accs[n % len(accs)]
+            c = (i * P) % WORD_PIECE
+            s = (i * P) % (S // 2)
+            nc.tensor.matmul_mx(
+                out=acc[:],
+                lhsT=tok_words[i * P // WORD_PIECE][:, c:c + P].bitcast(FP8X4),
+                lhsT_scale=tok_scales[i // half][:, s:s + P],
+                rhs=w_codes[d][:].bitcast(FP8X4),
+                rhs_scale=w_scales[d][:],
+                start=True,
+                stop=True,
+            )
+            acts[i, d] = keep.tile([P, PACK, P], F32, name=f"act{i}{d}")
+            nc.scalar.activation(acts[i, d][:], acc[:].rearrange("p (m t) -> p t m", t=PACK), GELU)
+
+        def mix(i):
+            turned[i] = psum.tile([P, PACK, P], F32, name="turned", tag="turned")
+            for d in range(D):
+                scaled = keep.tile([P, PACK, P], F32, name=f"scaled{i}{d}")
+                nc.vector.tensor_scalar(scaled[:], acts[i, d][:], gate_cols[:, i, d:d + 1], None, MULT)
+                for t in range(PACK):
+                    nc.tensor.matmul(
+                        turned[i][:, t, :], scaled[:, t, :], ident[:], is_transpose=True,
+                        start=(d == 0 and t == 0), stop=(d == D - 1 and t == PACK - 1),
+                    )
+
+        def drain(i):
+            group = [g for g in groups if i in g][0]
+            if i == group[0]:
+                ys[group] = keep.tile([P, PACK, len(group) * P], F32, name=f"y{i}")
+            a = i - group[0]
+            nc.scalar.copy(ys[group][:, :, a * P:(a + 1) * P], turned[i][:])
+            if i == group[-1]:
+                nc.sync.dma_start(out_rows[:, :, group[0] * P:(i + 1) * P], ys[group][:])
+
+        def pack(group):
+            cols = slice(group[0] * P, (group[-1] + 1) * P)
+            y_bf = keep.tile([P, PACK * P * len(group)], BF16, name=f"y_bf{group[0]}", align_bytes=64)
+            interleave(nc.vector.tensor_copy, y_bf[:], ys[group][:])
+            nc.vector.quantize_mx(out=y_codes[:, cols].bitcast(FP8X4), scales=y_scales[:, cols], in_=y_bf[:])
+            nc.sync.dma_start(out_words[:, cols], y_codes[:, cols].bitcast(I32))
+
+        last = {units.index((i, D - 1)): i for i in range(TILES)}
+        for n in range(len(units) + 3):
+            if n < len(units):
+                product(n)
+            if n == TILES + half:
+                turn_gates(0)
+                turn_gates(1)
+            if n in last:
+                mix(last[n])
+            if n - 3 in last:
+                drain(last[n - 3])
+        for group in groups:
+            pack(group)
+
+        for q in range(4):
+            nc.sync.dma_start(out_2[0, 4 * q:4 * q + 4, :].bitcast(I32), y_scales[32 * q:32 * q + 4, :].bitcast(I32))

@@ -16,6 +16,7 @@ U8 = mybir.dt.uint8
 FP8X4 = mybir.dt.float8_e4m3fn_x4
 GELU = mybir.ActivationFunctionType.Gelu_apprx_tanh
 MULT = mybir.AluOpType.mult
+ADD = mybir.AluOpType.add
 
 P = 128
 PACK = 4
@@ -37,7 +38,7 @@ def tile_picked_zsmoe_gelu_po_kernel(tc, x_words, x_scales, w1, w2, w3, gate, of
     weights = (w1, w2, w3)
     with ExitStack() as ctx:
         keep = ctx.enter_context(tc.tile_pool(name="keep", bufs=1))
-        psum = ctx.enter_context(tc.psum_pool(name="psum", bufs=4))
+        psum = ctx.enter_context(tc.psum_pool(name="psum", bufs=1))
 
         offsets = keep.tile([P, S // 16], U16, name="offsets")
         word_win = keep.tile([P, T], U32, name="word_win", align_bytes=64)
@@ -97,8 +98,11 @@ def tile_picked_zsmoe_gelu_po_kernel(tc, x_words, x_scales, w1, w2, w3, gate, of
 
         gate_cols = keep.tile([P, TILES, D], F32, name="gate_cols")
 
+        accs = [psum.tile([P, N], F32, name=f"acc{b}") for b in range(3)]
+        banks = [psum.tile([P, PACK, P], F32, name=f"bank{b}") for b in range(5)]
+
         def turn_gates(u):
-            bank = psum.tile([P, PACK, P], F32, name="turned", tag="turned")
+            bank = banks[u]
             for a in range(4):
                 i = 4 * u + a
                 nc.tensor.transpose(bank[:, a, :], gate_rows[:, i * P:(i + 1) * P], ident[:])
@@ -118,6 +122,8 @@ def tile_picked_zsmoe_gelu_po_kernel(tc, x_words, x_scales, w1, w2, w3, gate, of
             quantize_w(d, slice(0, N))
         gather_gates(0)
         gather_gates(1)
+        turn_gates(0)
+        turn_gates(1)
 
         y_codes = keep.tile([P, S], U32, name="y_codes", align_bytes=64)
         y_scales = keep.tile([P, S], U8, name="y_scales", align_bytes=64)
@@ -125,9 +131,8 @@ def tile_picked_zsmoe_gelu_po_kernel(tc, x_words, x_scales, w1, w2, w3, gate, of
         out_words = out_1[0].rearrange("p n t -> p (n t)").bitcast(I32)
 
         half = TILES // 2
-        accs = [psum.tile([P, N], F32, name=f"acc{b}", tag=f"acc{b}", bufs=1) for b in range(4)]
-        units = [(i, 0) for i in range(TILES)] + [(i, d) for d in (1, 2) for i in range(half)]
-        units = units + [(i, d) for i in range(half, TILES) for d in (1, 2)]
+        units = [(i, 0) for i in range(8)] + [(i, 1) for i in range(4)]
+        units = units + [(i, d) for i in range(TILES) for d in range(D) if (i, d) not in units]
         groups = [(0, 1), (2, 3), (4, 5), (6,), (7,)]
 
         acts = {}
@@ -153,15 +158,22 @@ def tile_picked_zsmoe_gelu_po_kernel(tc, x_words, x_scales, w1, w2, w3, gate, of
             nc.scalar.activation(acts[i, d][:], acc[:].rearrange("p (m t) -> p t m", t=PACK), GELU)
 
         def mix(i):
-            turned[i] = psum.tile([P, PACK, P], F32, name="turned", tag="turned")
+            turned[i] = banks[(i + 2) % len(banks)]
+            merged = i >= 0
             for d in range(D):
-                scaled = keep.tile([P, PACK, P], F32, name=f"scaled{i}{d}")
-                nc.vector.tensor_scalar(scaled[:], acts[i, d][:], gate_cols[:, i, d:d + 1], None, MULT)
-                for t in range(PACK):
-                    nc.tensor.matmul(
-                        turned[i][:, t, :], scaled[:, t, :], ident[:], is_transpose=True,
-                        start=(d == 0 and t == 0), stop=(d == D - 1 and t == PACK - 1),
-                    )
+                scaled[d] = keep.tile([P, PACK * P], F32, name=f"scaled{i}{d}")
+                act = acts[i, d][:].rearrange("p t m -> p (t m)")
+                if merged and d == 1:
+                    nc.vector.scalar_tensor_tensor(scaled[d][:], act, gate_cols[:, i, d:d + 1], scaled[0][:], MULT, ADD)
+                else:
+                    nc.vector.tensor_scalar(scaled[d][:], act, gate_cols[:, i, d:d + 1], None, MULT)
+                first = 1 if merged else 0
+                if d >= first:
+                    for t in range(PACK):
+                        nc.tensor.matmul(
+                            turned[i][:, t, :], scaled[d][:, t * P:(t + 1) * P], ident[:], is_transpose=True,
+                            start=(d == first and t == 0), stop=(d == D - 1 and t == PACK - 1),
+                        )
 
         def drain(i):
             group = [g for g in groups if i in g][0]
@@ -179,19 +191,19 @@ def tile_picked_zsmoe_gelu_po_kernel(tc, x_words, x_scales, w1, w2, w3, gate, of
             nc.vector.quantize_mx(out=y_codes[:, cols].bitcast(FP8X4), scales=y_scales[:, cols], in_=y_bf[:])
             nc.sync.dma_start(out_words[:, cols], y_codes[:, cols].bitcast(I32))
 
-        last = {units.index((i, D - 1)): i for i in range(TILES)}
-        for n in range(len(units) + 3):
+        place = []
+        for i in range(TILES):
+            place.append(max([units.index((i, D - 1)) + 2] + [p + 2 for p in place[-1:]]))
+        for n in range(place[-1] + 3 + 1):
             if n < len(units):
                 product(n)
-            if n == TILES + half:
-                turn_gates(0)
-                turn_gates(1)
-            if n in last:
-                mix(last[n])
-            if n - 3 in last:
-                drain(last[n - 3])
-        for group in groups:
-            pack(group)
+            if n in place:
+                mix(place.index(n))
+            if n - 1 in place:
+                drain(place.index(n - 1))
+            for group in groups:
+                if place[group[-1]] + 3 == n:
+                    pack(group)
 
         for q in range(4):
-            nc.sync.dma_start(out_2[0, 4 * q:4 * q + 4, :].bitcast(I32), y_scales[32 * q:32 * q + 4, :].bitcast(I32))
+            (nc.sync, nc.scalar)[q % 2].dma_start(out_2[0, 4 * q:4 * q + 4, :].bitcast(I32), y_scales[32 * q:32 * q + 4, :].bitcast(I32))

@@ -4,8 +4,14 @@ import concourse.mybir as mybir
 from concourse.masks import make_identity
 
 K, T, S, D, N = 512, 2048, 1024, 3, 512
+P = 128
+PACK = 4
+QUADRANTS = 4
+LIST_ROWS = 16
+TILES = S // P
+
 FLOPS = 2 * D * K * N * S
-BYTES = K * T + 16 * T + D * K * N * 4 + D * T * 4 + 128 * (S // 16) * 2 + N * S * 4 + N * S + 16 * S
+BYTES = K * T + K // 32 * T + 4 * D * K * N + 4 * D * T + 2 * P * S // LIST_ROWS + 4 * N * S + N * S + N // 32 * S
 
 F32 = mybir.dt.float32
 BF16 = mybir.dt.bfloat16
@@ -18,12 +24,17 @@ GELU = mybir.ActivationFunctionType.Gelu_apprx_tanh
 MULT = mybir.AluOpType.mult
 ADD = mybir.AluOpType.add
 
-P = 128
-PACK = 4
-TILES = S // P
-HALF = N // 2
-GATE_STEP = 4
+W1_PARTS = (slice(0, 128), slice(128, 320), slice(320, N))
+GATE_ROWS = slice(4, 4 * (D + 1), 4)
 WORD_PIECE = 256
+GATE_PIECE = PACK * P
+ACC_BANKS = 4
+TURN_BANKS = 8 - ACC_BANKS
+SECOND_LAYER_LEAD = 5
+VECTOR_SUM_FROM = 5
+MIX_LAG = 2
+PACK_LAG = 3
+GROUPS = ((0, 1), (2, 3), (4, 5), (6,), (7,))
 
 
 def interleave(copy, dst, src):
@@ -35,39 +46,37 @@ def interleave(copy, dst, src):
 
 def tile_picked_zsmoe_gelu_po_kernel(tc, x_words, x_scales, w1, w2, w3, gate, offs, out_0, out_1, out_2):
     nc = tc.nc
-    weights = (w1, w2, w3)
     with ExitStack() as ctx:
         keep = ctx.enter_context(tc.tile_pool(name="keep", bufs=1))
         psum = ctx.enter_context(tc.psum_pool(name="psum", bufs=1))
 
-        offsets = keep.tile([P, S // 16], U16, name="offsets")
-        word_win = keep.tile([P, T], U32, name="word_win", align_bytes=64)
-        scale_win = keep.tile([P, T], U8, name="scale_win", align_bytes=64)
-        gate_win = keep.tile([P, T], F32, name="gate_win", align_bytes=64)
+        offsets = keep.tile([P, S // LIST_ROWS], U16, name="offsets")
+        word_window = keep.tile([P, T], U32, name="word_window", align_bytes=64)
+        scale_window = keep.tile([P, T], U8, name="scale_window", align_bytes=64)
+        gate_window = keep.tile([P, T], F32, name="gate_window", align_bytes=64)
         ident = keep.tile([P, P], F32, name="ident", align_bytes=64)
         warm = keep.tile([P, 2], F32, name="warm")
 
         nc.vector.memset(warm[:, 0:1], 0.0)
-        nc.vector.memset(scale_win[:].bitcast(I32), 0)
-        nc.vector.memset(gate_win[:], 0.0)
+        nc.gpsimd.memset(scale_window[:].bitcast(I32), 0)
+        nc.vector.memset(gate_window[:], 0.0)
         make_identity(nc, ident[:])
 
+        def load_weight(w, cols, name):
+            raw = keep.tile([P, PACK, cols.stop - cols.start], F32, name=name, align_bytes=64)
+            nc.sync.dma_start(raw[:], w[:, cols].rearrange("(p t) m -> p t m", t=PACK))
+            return raw
+
         nc.sync.dma_start(offsets[:], offs)
-        w_raw = {}
-
-        def load_w1(h):
-            w_raw[0, h] = keep.tile([P, PACK, HALF], F32, name=f"w_raw0{h}", align_bytes=64)
-            nc.sync.dma_start(w_raw[0, h][:], w1[:, h * HALF:(h + 1) * HALF].rearrange("(p t) m -> p t m", t=PACK))
-
-        load_w1(0)
-        for q in range(4):
-            nc.sync.dma_start(scale_win[32 * q:32 * q + 4, :].bitcast(I32), x_scales[0, 4 * q:4 * q + 4, :].bitcast(I32))
-        load_w1(1)
-        nc.sync.dma_start(word_win[:].bitcast(I32), x_words[0].rearrange("p n t -> p (n t)").bitcast(I32))
-        for d in (1, 2):
-            w_raw[d] = keep.tile([P, PACK, N], F32, name=f"w_raw{d}", align_bytes=64)
-            nc.sync.dma_start(w_raw[d][:], weights[d].rearrange("(p t) m -> p t m", t=PACK))
-        nc.sync.dma_start(gate_win[GATE_STEP:GATE_STEP * (D + 1):GATE_STEP, :], gate[:, 0, :])
+        w1_raw = [load_weight(w1, W1_PARTS[0], "w1_raw0")]
+        for q in range(QUADRANTS):
+            nc.sync.dma_start(
+                scale_window[32 * q:32 * q + 4, :].bitcast(I32), x_scales[0, 4 * q:4 * q + 4, :].bitcast(I32)
+            )
+        w1_raw.extend(load_weight(w1, W1_PARTS[a], f"w1_raw{a}") for a in range(1, len(W1_PARTS)))
+        nc.sync.dma_start(word_window[:].bitcast(I32), x_words[0].rearrange("p n t -> p (n t)").bitcast(I32))
+        later_raw = [load_weight(w, slice(0, N), f"w{d + 2}_raw") for d, w in enumerate((w2, w3))]
+        nc.sync.dma_start(gate_window[GATE_ROWS, :], gate[:, 0, :])
 
         nc.scalar.activation(warm[:, 1:2], warm[:, 0:1], GELU)
 
@@ -75,80 +84,66 @@ def tile_picked_zsmoe_gelu_po_kernel(tc, x_words, x_scales, w1, w2, w3, gate, of
         w_codes = [keep.tile([P, N], U32, name=f"w_codes{d}", align_bytes=64) for d in range(D)]
         w_scales = [keep.tile([P, N], U8, name=f"w_scales{d}", align_bytes=64) for d in range(D)]
 
-        def quantize_w(d, cols):
-            nc.vector.quantize_mx(
-                out=w_codes[d][:, cols].bitcast(FP8X4),
-                scales=w_scales[d][:, cols],
-                in_=w_bf[d][:, PACK * cols.start:PACK * cols.stop],
-            )
+        def quantize_weight(d):
+            nc.vector.quantize_mx(out=w_codes[d][:].bitcast(FP8X4), scales=w_scales[d][:], in_=w_bf[d][:])
 
-        for h in range(2):
-            interleave(nc.scalar.copy, w_bf[0][:, h * PACK * HALF:(h + 1) * PACK * HALF], w_raw[0, h][:])
+        def entries(first, count):
+            return offsets[:, first // LIST_ROWS:(first + count) // LIST_ROWS]
+
+        for raw, cols in zip(w1_raw, W1_PARTS):
+            interleave(nc.scalar.copy, w_bf[0][:, PACK * cols.start:PACK * cols.stop], raw[:])
+
+        token_scales = keep.tile([P, S], U8, name="token_scales", align_bytes=64)
+        nc.vector.tensor_copy(token_scales[:], scale_window[:].indirect(offsets[:]))
+        quantize_weight(0)
+
+        token_words = []
+        for first in range(0, S, WORD_PIECE):
+            token_words.append(keep.tile([P, WORD_PIECE], U32, name=f"token_words{first}", align_bytes=64))
+            nc.vector.tensor_copy(token_words[-1][:], word_window[:].indirect(entries(first, WORD_PIECE)))
+
+        for d in range(1, D):
+            interleave(nc.vector.tensor_copy, w_bf[d][:], later_raw[d - 1][:])
+            quantize_weight(d)
+
+        accs = [psum.tile([P, N], F32, name=f"acc{b}") for b in range(ACC_BANKS)]
+        turns = [psum.tile([P, PACK, P], F32, name=f"turn{b}") for b in range(TURN_BANKS)]
 
         gate_rows = keep.tile([P, S], F32, name="gate_rows", align_bytes=64)
-
-        tok_scales = [keep.tile([P, S // 2], U8, name=f"tok_scales{u}", align_bytes=64) for u in range(2)]
-        tok_words = [keep.tile([P, WORD_PIECE], U32, name=f"tok_words{u}", align_bytes=64) for u in range(S // WORD_PIECE)]
-
-        def gather_scales(u):
-            nc.vector.tensor_copy(tok_scales[u][:], scale_win[:].indirect(offsets[:, 32 * u:32 * (u + 1)]))
-
-        def gather_words(u):
-            nc.vector.tensor_copy(tok_words[u][:], word_win[:].indirect(offsets[:, 16 * u:16 * (u + 1)]))
-
-        gate_cols = keep.tile([P, TILES, D], F32, name="gate_cols")
-
-        accs = [psum.tile([P, N], F32, name=f"acc{b}") for b in range(3)]
-        banks = [psum.tile([P, PACK, P], F32, name=f"bank{b}") for b in range(5)]
-
-        def turn_gates(u):
-            bank = banks[u]
-            for a in range(4):
-                i = 4 * u + a
-                nc.tensor.transpose(bank[:, a, :], gate_rows[:, i * P:(i + 1) * P], ident[:])
-            nc.vector.tensor_copy(gate_cols[:, 4 * u:4 * u + 4, :], bank[:, :, GATE_STEP:GATE_STEP * (D + 1):GATE_STEP])
-
-        def gather_gates(u):
-            nc.vector.tensor_copy(gate_rows[:, u * (S // 2):(u + 1) * (S // 2)], gate_win[:].indirect(offsets[:, 32 * u:32 * (u + 1)]))
-
-        gather_scales(0)
-        gather_scales(1)
-        quantize_w(0, slice(0, HALF))
-        quantize_w(0, slice(HALF, N))
-        for u in range(S // WORD_PIECE):
-            gather_words(u)
-        for d in (1, 2):
-            interleave(nc.vector.tensor_copy, w_bf[d][:], w_raw[d][:])
-            quantize_w(d, slice(0, N))
-        gather_gates(0)
-        gather_gates(1)
-        turn_gates(0)
-        turn_gates(1)
+        gates = keep.tile([P, TILES, D], F32, name="gates")
+        gate_pieces = S // GATE_PIECE
+        for u in range(gate_pieces):
+            nc.vector.tensor_copy(
+                gate_rows[:, u * GATE_PIECE:(u + 1) * GATE_PIECE],
+                gate_window[:].indirect(entries(u * GATE_PIECE, GATE_PIECE)),
+            )
+        for u in range(gate_pieces):
+            for a in range(PACK):
+                i = PACK * u + a
+                nc.tensor.transpose(turns[u][:, a, :], gate_rows[:, i * P:(i + 1) * P], ident[:])
+            nc.vector.tensor_copy(gates[:, PACK * u:PACK * (u + 1), :], turns[u][:, :, GATE_ROWS])
 
         y_codes = keep.tile([P, S], U32, name="y_codes", align_bytes=64)
         y_scales = keep.tile([P, S], U8, name="y_scales", align_bytes=64)
         out_rows = out_0.rearrange("(p t) j -> p t j", t=PACK)
         out_words = out_1[0].rearrange("p n t -> p (n t)").bitcast(I32)
 
-        half = TILES // 2
-        units = [(i, 0) for i in range(8)] + [(i, 1) for i in range(4)]
-        units = units + [(i, d) for i in range(TILES) for d in range(D) if (i, d) not in units]
-        groups = [(0, 1), (2, 3), (4, 5), (6,), (7,)]
-
+        early = [(i, 0) for i in range(TILES)] + [(i, 1) for i in range(SECOND_LAYER_LEAD)]
+        units = early + [(i, d) for i in range(TILES) for d in range(D) if (i, d) not in early]
         acts = {}
-        scaled = {}
-        turned = {}
         ys = {}
+
+        def turn_bank(i):
+            return turns[(gate_pieces + i) % TURN_BANKS]
 
         def product(n):
             i, d = units[n]
-            acc = accs[n % len(accs)]
-            c = (i * P) % WORD_PIECE
-            s = (i * P) % (S // 2)
+            acc = accs[n % ACC_BANKS]
+            c = i * P % WORD_PIECE
             nc.tensor.matmul_mx(
                 out=acc[:],
-                lhsT=tok_words[i * P // WORD_PIECE][:, c:c + P].bitcast(FP8X4),
-                lhsT_scale=tok_scales[i // half][:, s:s + P],
+                lhsT=token_words[i * P // WORD_PIECE][:, c:c + P].bitcast(FP8X4),
+                lhsT_scale=token_scales[:, i * P:(i + 1) * P],
                 rhs=w_codes[d][:].bitcast(FP8X4),
                 rhs_scale=w_scales[d][:],
                 start=True,
@@ -158,29 +153,33 @@ def tile_picked_zsmoe_gelu_po_kernel(tc, x_words, x_scales, w1, w2, w3, gate, of
             nc.scalar.activation(acts[i, d][:], acc[:].rearrange("p (m t) -> p t m", t=PACK), GELU)
 
         def mix(i):
-            turned[i] = banks[(i + 2) % len(banks)]
-            merged = i >= 0
+            first_turned = 1 if i >= VECTOR_SUM_FROM else 0
+            gated = []
             for d in range(D):
-                scaled[d] = keep.tile([P, PACK * P], F32, name=f"scaled{i}{d}")
+                gated.append(keep.tile([P, PACK * P], F32, name=f"gated{i}{d}"))
                 act = acts[i, d][:].rearrange("p t m -> p (t m)")
-                if merged and d == 1:
-                    nc.vector.scalar_tensor_tensor(scaled[d][:], act, gate_cols[:, i, d:d + 1], scaled[0][:], MULT, ADD)
-                else:
-                    nc.vector.tensor_scalar(scaled[d][:], act, gate_cols[:, i, d:d + 1], None, MULT)
-                first = 1 if merged else 0
-                if d >= first:
+                nc.vector.tensor_scalar(gated[d][:], act, gates[:, i, d:d + 1], None, MULT)
+                term = gated[d]
+                if d == first_turned == 1:
+                    term = keep.tile([P, PACK * P], F32, name=f"summed{i}")
+                    nc.vector.tensor_tensor(term[:], gated[0][:], gated[1][:], ADD)
+                if d >= first_turned:
                     for t in range(PACK):
                         nc.tensor.matmul(
-                            turned[i][:, t, :], scaled[d][:, t * P:(t + 1) * P], ident[:], is_transpose=True,
-                            start=(d == first and t == 0), stop=(d == D - 1 and t == PACK - 1),
+                            turn_bank(i)[:, t, :],
+                            term[:, t * P:(t + 1) * P],
+                            ident[:],
+                            is_transpose=True,
+                            start=(d == first_turned and t == 0),
+                            stop=(d == D - 1 and t == PACK - 1),
                         )
 
         def drain(i):
-            group = [g for g in groups if i in g][0]
+            group = [g for g in GROUPS if i in g][0]
             if i == group[0]:
                 ys[group] = keep.tile([P, PACK, len(group) * P], F32, name=f"y{i}")
-            a = i - group[0]
-            nc.scalar.copy(ys[group][:, :, a * P:(a + 1) * P], turned[i][:])
+            c = (i - group[0]) * P
+            nc.scalar.copy(ys[group][:, :, c:c + P], turn_bank(i)[:])
             if i == group[-1]:
                 nc.sync.dma_start(out_rows[:, :, group[0] * P:(i + 1) * P], ys[group][:])
 
@@ -189,21 +188,24 @@ def tile_picked_zsmoe_gelu_po_kernel(tc, x_words, x_scales, w1, w2, w3, gate, of
             y_bf = keep.tile([P, PACK * P * len(group)], BF16, name=f"y_bf{group[0]}", align_bytes=64)
             interleave(nc.vector.tensor_copy, y_bf[:], ys[group][:])
             nc.vector.quantize_mx(out=y_codes[:, cols].bitcast(FP8X4), scales=y_scales[:, cols], in_=y_bf[:])
-            nc.sync.dma_start(out_words[:, cols], y_codes[:, cols].bitcast(I32))
+            if group != GROUPS[-2]:
+                first = GROUPS[-2][0] * P if group == GROUPS[-1] else cols.start
+                nc.sync.dma_start(out_words[:, first:cols.stop], y_codes[:, first:cols.stop].bitcast(I32))
 
-        place = []
+        mix_at = []
         for i in range(TILES):
-            place.append(max([units.index((i, D - 1)) + 2] + [p + 2 for p in place[-1:]]))
-        for n in range(place[-1] + 3 + 1):
+            mix_at.append(max([units.index((i, D - 1))] + mix_at[-1:]) + MIX_LAG)
+        for n in range(mix_at[-1] + PACK_LAG + 1):
             if n < len(units):
                 product(n)
-            if n in place:
-                mix(place.index(n))
-            if n - 1 in place:
-                drain(place.index(n - 1))
-            for group in groups:
-                if place[group[-1]] + 3 == n:
+            if n in mix_at:
+                mix(mix_at.index(n))
+            if n - 1 in mix_at:
+                drain(mix_at.index(n - 1))
+            for group in GROUPS:
+                if n == mix_at[group[-1]] + PACK_LAG:
                     pack(group)
 
-        for q in range(4):
-            (nc.sync, nc.scalar)[q % 2].dma_start(out_2[0, 4 * q:4 * q + 4, :].bitcast(I32), y_scales[32 * q:32 * q + 4, :].bitcast(I32))
+        for q in range(QUADRANTS):
+            queue = (nc.sync, nc.scalar)[q % 2]
+            queue.dma_start(out_2[0, 4 * q:4 * q + 4, :].bitcast(I32), y_scales[32 * q:32 * q + 4, :].bitcast(I32))

@@ -25,13 +25,14 @@ MULT = mybir.AluOpType.mult
 ADD = mybir.AluOpType.add
 
 W1_PARTS = (slice(0, 128), slice(128, 320), slice(320, N))
+W2_PARTS = (slice(0, 128), slice(128, N))
 GATE_ROWS = slice(4, 4 * (D + 1), 4)
 WORD_PIECE = 256
 GATE_PIECE = PACK * P
 ACC_BANKS = 4
 TURN_BANKS = 8 - ACC_BANKS
-SECOND_LAYER_LEAD = 5
-VECTOR_SUM_FROM = 5
+SECOND_LAYER_LEAD = 6
+VECTOR_SUM_FROM = 3
 MIX_LAG = 2
 PACK_LAG = 3
 GROUPS = ((0, 1), (2, 3), (4, 5), (6,), (7,))
@@ -39,8 +40,8 @@ GROUPS = ((0, 1), (2, 3), (4, 5), (6,), (7,))
 
 def interleave(copy, dst, src):
     copy(
-        out=dst.rearrange("p (c i t) -> p c t i", i=4, t=PACK),
-        in_=src.rearrange("p t (c i) -> p c t i", i=4),
+        out=dst.rearrange("p (c i t) -> p c t i", i=2, t=PACK),
+        in_=src.rearrange("p t (c i) -> p c t i", i=2),
     )
 
 
@@ -75,7 +76,8 @@ def tile_picked_zsmoe_gelu_po_kernel(tc, x_words, x_scales, w1, w2, w3, gate, of
             )
         w1_raw.extend(load_weight(w1, W1_PARTS[a], f"w1_raw{a}") for a in range(1, len(W1_PARTS)))
         nc.sync.dma_start(word_window[:].bitcast(I32), x_words[0].rearrange("p n t -> p (n t)").bitcast(I32))
-        later_raw = [load_weight(w, slice(0, N), f"w{d + 2}_raw") for d, w in enumerate((w2, w3))]
+        w2_raw = [load_weight(w2, cols, f"w2_raw{a}") for a, cols in enumerate(W2_PARTS)]
+        w3_raw = load_weight(w3, slice(0, N), "w3_raw")
         nc.sync.dma_start(gate_window[GATE_ROWS, :], gate[:, 0, :])
 
         nc.scalar.activation(warm[:, 1:2], warm[:, 0:1], GELU)
@@ -90,8 +92,11 @@ def tile_picked_zsmoe_gelu_po_kernel(tc, x_words, x_scales, w1, w2, w3, gate, of
         def entries(first, count):
             return offsets[:, first // LIST_ROWS:(first + count) // LIST_ROWS]
 
+        def round_weight(copy, d, raw, cols):
+            interleave(copy, w_bf[d][:, PACK * cols.start:PACK * cols.stop], raw[:])
+
         for raw, cols in zip(w1_raw, W1_PARTS):
-            interleave(nc.scalar.copy, w_bf[0][:, PACK * cols.start:PACK * cols.stop], raw[:])
+            round_weight(nc.scalar.copy, 0, raw, cols)
 
         token_scales = keep.tile([P, S], U8, name="token_scales", align_bytes=64)
         nc.vector.tensor_copy(token_scales[:], scale_window[:].indirect(offsets[:]))
@@ -102,9 +107,11 @@ def tile_picked_zsmoe_gelu_po_kernel(tc, x_words, x_scales, w1, w2, w3, gate, of
             token_words.append(keep.tile([P, WORD_PIECE], U32, name=f"token_words{first}", align_bytes=64))
             nc.vector.tensor_copy(token_words[-1][:], word_window[:].indirect(entries(first, WORD_PIECE)))
 
-        for d in range(1, D):
-            interleave(nc.vector.tensor_copy, w_bf[d][:], later_raw[d - 1][:])
-            quantize_weight(d)
+        round_weight(nc.scalar.copy, 1, w2_raw[0], W2_PARTS[0])
+        round_weight(nc.vector.tensor_copy, 1, w2_raw[1], W2_PARTS[1])
+        quantize_weight(1)
+        round_weight(nc.vector.tensor_copy, 2, w3_raw, slice(0, N))
+        quantize_weight(2)
 
         accs = [psum.tile([P, N], F32, name=f"acc{b}") for b in range(ACC_BANKS)]
         turns = [psum.tile([P, PACK, P], F32, name=f"turn{b}") for b in range(TURN_BANKS)]
@@ -158,16 +165,15 @@ def tile_picked_zsmoe_gelu_po_kernel(tc, x_words, x_scales, w1, w2, w3, gate, of
             for d in range(D):
                 gated.append(keep.tile([P, PACK * P], F32, name=f"gated{i}{d}"))
                 act = acts[i, d][:].rearrange("p t m -> p (t m)")
-                nc.vector.tensor_scalar(gated[d][:], act, gates[:, i, d:d + 1], None, MULT)
-                term = gated[d]
                 if d == first_turned == 1:
-                    term = keep.tile([P, PACK * P], F32, name=f"summed{i}")
-                    nc.vector.tensor_tensor(term[:], gated[0][:], gated[1][:], ADD)
+                    nc.vector.scalar_tensor_tensor(gated[d][:], act, gates[:, i, d:d + 1], gated[0][:], MULT, ADD)
+                else:
+                    nc.vector.tensor_scalar(gated[d][:], act, gates[:, i, d:d + 1], None, MULT)
                 if d >= first_turned:
                     for t in range(PACK):
                         nc.tensor.matmul(
                             turn_bank(i)[:, t, :],
-                            term[:, t * P:(t + 1) * P],
+                            gated[d][:, t * P:(t + 1) * P],
                             ident[:],
                             is_transpose=True,
                             start=(d == first_turned and t == 0),

@@ -27,7 +27,7 @@ ADD = mybir.AluOpType.add
 W1_PARTS = (slice(0, 128), slice(128, 320), slice(320, N))
 W2_PARTS = (slice(0, 128), slice(128, N))
 GATE_ROWS = slice(4, 4 * (D + 1), 4)
-WORD_PIECE = 256
+WORD_PIECES = ((0, 256), (256, 256), (512, 512))
 GATE_PIECE = PACK * P
 ACC_BANKS = 4
 TURN_BANKS = 8 - ACC_BANKS
@@ -35,13 +35,14 @@ SECOND_LAYER_LEAD = 6
 VECTOR_SUM_FROM = 3
 MIX_LAG = 2
 PACK_LAG = 3
+PAIR = 2
 GROUPS = ((0, 1), (2, 3), (4, 5), (6,), (7,))
 
 
 def interleave(copy, dst, src):
     copy(
-        out=dst.rearrange("p (c i t) -> p c t i", i=2, t=PACK),
-        in_=src.rearrange("p t (c i) -> p c t i", i=2),
+        out=dst.rearrange("p (c i t) -> p c t i", i=4, t=PACK),
+        in_=src.rearrange("p t (c i) -> p c t i", i=4),
     )
 
 
@@ -102,10 +103,9 @@ def tile_picked_zsmoe_gelu_po_kernel(tc, x_words, x_scales, w1, w2, w3, gate, of
         nc.vector.tensor_copy(token_scales[:], scale_window[:].indirect(offsets[:]))
         quantize_weight(0)
 
-        token_words = []
-        for first in range(0, S, WORD_PIECE):
-            token_words.append(keep.tile([P, WORD_PIECE], U32, name=f"token_words{first}", align_bytes=64))
-            nc.vector.tensor_copy(token_words[-1][:], word_window[:].indirect(entries(first, WORD_PIECE)))
+        token_words = keep.tile([P, S], U32, name="token_words", align_bytes=64)
+        for first, count in WORD_PIECES:
+            nc.vector.tensor_copy(token_words[:, first:first + count], word_window[:].indirect(entries(first, count)))
 
         round_weight(nc.scalar.copy, 1, w2_raw[0], W2_PARTS[0])
         round_weight(nc.vector.tensor_copy, 1, w2_raw[1], W2_PARTS[1])
@@ -138,7 +138,7 @@ def tile_picked_zsmoe_gelu_po_kernel(tc, x_words, x_scales, w1, w2, w3, gate, of
         early = [(i, 0) for i in range(TILES)] + [(i, 1) for i in range(SECOND_LAYER_LEAD)]
         units = early + [(i, d) for i in range(TILES) for d in range(D) if (i, d) not in early]
         acts = {}
-        ys = {}
+        ys = [keep.tile([P, PACK, PAIR * P], F32, name=f"y{pair}") for pair in range(TILES // PAIR)]
 
         def turn_bank(i):
             return turns[(gate_pieces + i) % TURN_BANKS]
@@ -146,10 +146,9 @@ def tile_picked_zsmoe_gelu_po_kernel(tc, x_words, x_scales, w1, w2, w3, gate, of
         def product(n):
             i, d = units[n]
             acc = accs[n % ACC_BANKS]
-            c = i * P % WORD_PIECE
             nc.tensor.matmul_mx(
                 out=acc[:],
-                lhsT=token_words[i * P // WORD_PIECE][:, c:c + P].bitcast(FP8X4),
+                lhsT=token_words[:, i * P:(i + 1) * P].bitcast(FP8X4),
                 lhsT_scale=token_scales[:, i * P:(i + 1) * P],
                 rhs=w_codes[d][:].bitcast(FP8X4),
                 rhs_scale=w_scales[d][:],
@@ -181,18 +180,17 @@ def tile_picked_zsmoe_gelu_po_kernel(tc, x_words, x_scales, w1, w2, w3, gate, of
                         )
 
         def drain(i):
-            group = [g for g in GROUPS if i in g][0]
-            if i == group[0]:
-                ys[group] = keep.tile([P, PACK, len(group) * P], F32, name=f"y{i}")
-            c = (i - group[0]) * P
-            nc.scalar.copy(ys[group][:, :, c:c + P], turn_bank(i)[:])
-            if i == group[-1]:
-                nc.sync.dma_start(out_rows[:, :, group[0] * P:(i + 1) * P], ys[group][:])
+            pair, place = divmod(i, PAIR)
+            nc.scalar.copy(ys[pair][:, :, place * P:(place + 1) * P], turn_bank(i)[:])
+            if place == PAIR - 1:
+                nc.sync.dma_start(out_rows[:, :, pair * PAIR * P:(i + 1) * P], ys[pair][:])
 
         def pack(group):
             cols = slice(group[0] * P, (group[-1] + 1) * P)
+            pair, place = divmod(group[0], PAIR)
+            y = ys[pair][:, :, place * P:(place + len(group)) * P]
             y_bf = keep.tile([P, PACK * P * len(group)], BF16, name=f"y_bf{group[0]}", align_bytes=64)
-            interleave(nc.vector.tensor_copy, y_bf[:], ys[group][:])
+            interleave(nc.scalar.copy if group == GROUPS[-1] else nc.vector.tensor_copy, y_bf[:], y)
             nc.vector.quantize_mx(out=y_codes[:, cols].bitcast(FP8X4), scales=y_scales[:, cols], in_=y_bf[:])
             if group != GROUPS[-2]:
                 first = GROUPS[-2][0] * P if group == GROUPS[-1] else cols.start

@@ -24,7 +24,7 @@ GELU = mybir.ActivationFunctionType.Gelu_apprx_tanh
 MULT = mybir.AluOpType.mult
 ADD = mybir.AluOpType.add
 
-W1_PARTS = (slice(0, 128), slice(128, 320), slice(320, N))
+W1_PARTS = (slice(0, 256), slice(256, 384), slice(384, N))
 W2_PARTS = (slice(0, 128), slice(128, N))
 GATE_ROWS = slice(4, 4 * (D + 1), 4)
 WORD_PIECES = ((0, 256), (256, 256), (512, 512))
@@ -59,26 +59,24 @@ def tile_picked_zsmoe_gelu_po_kernel(tc, x_words, x_scales, w1, w2, w3, gate, of
         ident = keep.tile([P, P], F32, name="ident", align_bytes=64)
         warm = keep.tile([P, 2], F32, name="warm")
 
+        nc.vector.memset(scale_window[:].bitcast(I32), 0)
         nc.vector.memset(warm[:, 0:1], 0.0)
-        nc.gpsimd.memset(scale_window[:].bitcast(I32), 0)
         nc.vector.memset(gate_window[:], 0.0)
         make_identity(nc, ident[:])
 
-        def load_weight(w, cols, name):
-            raw = keep.tile([P, PACK, cols.stop - cols.start], F32, name=name, align_bytes=64)
-            nc.sync.dma_start(raw[:], w[:, cols].rearrange("(p t) m -> p t m", t=PACK))
-            return raw
+        w_raw = [keep.tile([P, PACK, N], F32, name=f"w_raw{d}", align_bytes=64) for d in range(D)]
+
+        def load_weight(d, rows):
+            nc.sync.dma_start(w_raw[d][:, rows, :], (w1, w2, w3)[d].rearrange("(p t) m -> p t m", t=PACK)[:, rows, :])
 
         nc.sync.dma_start(offsets[:], offs)
-        w1_raw = [load_weight(w1, W1_PARTS[0], "w1_raw0")]
-        for q in range(QUADRANTS):
-            nc.sync.dma_start(
-                scale_window[32 * q:32 * q + 4, :].bitcast(I32), x_scales[0, 4 * q:4 * q + 4, :].bitcast(I32)
-            )
-        w1_raw.extend(load_weight(w1, W1_PARTS[a], f"w1_raw{a}") for a in range(1, len(W1_PARTS)))
+        load_weight(0, slice(0, 1))
+        for r in range(4):
+            nc.sync.dma_start(scale_window[r:P:32, :].bitcast(I32), x_scales[0, r:16:4, :].bitcast(I32))
+        load_weight(0, slice(1, PACK))
         nc.sync.dma_start(word_window[:].bitcast(I32), x_words[0].rearrange("p n t -> p (n t)").bitcast(I32))
-        w2_raw = [load_weight(w2, cols, f"w2_raw{a}") for a, cols in enumerate(W2_PARTS)]
-        w3_raw = load_weight(w3, slice(0, N), "w3_raw")
+        load_weight(1, slice(0, PACK))
+        load_weight(2, slice(0, PACK))
         nc.sync.dma_start(gate_window[GATE_ROWS, :], gate[:, 0, :])
 
         nc.scalar.activation(warm[:, 1:2], warm[:, 0:1], GELU)
@@ -87,31 +85,41 @@ def tile_picked_zsmoe_gelu_po_kernel(tc, x_words, x_scales, w1, w2, w3, gate, of
         w_codes = [keep.tile([P, N], U32, name=f"w_codes{d}", align_bytes=64) for d in range(D)]
         w_scales = [keep.tile([P, N], U8, name=f"w_scales{d}", align_bytes=64) for d in range(D)]
 
-        def quantize_weight(d):
-            nc.vector.quantize_mx(out=w_codes[d][:].bitcast(FP8X4), scales=w_scales[d][:], in_=w_bf[d][:])
+        def quantize_weight(d, cols):
+            nc.vector.quantize_mx(
+                out=w_codes[d][:, cols].bitcast(FP8X4),
+                scales=w_scales[d][:, cols],
+                in_=w_bf[d][:, PACK * cols.start:PACK * cols.stop],
+            )
 
         def entries(first, count):
             return offsets[:, first // LIST_ROWS:(first + count) // LIST_ROWS]
 
-        def round_weight(copy, d, raw, cols):
-            interleave(copy, w_bf[d][:, PACK * cols.start:PACK * cols.stop], raw[:])
+        def round_weight(copy, d, cols):
+            interleave(copy, w_bf[d][:, PACK * cols.start:PACK * cols.stop], w_raw[d][:, :, cols])
 
-        for raw, cols in zip(w1_raw, W1_PARTS):
-            round_weight(nc.scalar.copy, 0, raw, cols)
+        for cols in W1_PARTS[:2]:
+            round_weight(nc.scalar.copy, 0, cols)
 
         token_scales = keep.tile([P, S], U8, name="token_scales", align_bytes=64)
         nc.vector.tensor_copy(token_scales[:], scale_window[:].indirect(offsets[:]))
-        quantize_weight(0)
-
         token_words = keep.tile([P, S], U32, name="token_words", align_bytes=64)
-        for first, count in WORD_PIECES:
+
+        def gather_words(first, count):
             nc.vector.tensor_copy(token_words[:, first:first + count], word_window[:].indirect(entries(first, count)))
 
-        round_weight(nc.scalar.copy, 1, w2_raw[0], W2_PARTS[0])
-        round_weight(nc.vector.tensor_copy, 1, w2_raw[1], W2_PARTS[1])
-        quantize_weight(1)
-        round_weight(nc.vector.tensor_copy, 2, w3_raw, slice(0, N))
-        quantize_weight(2)
+        quantize_weight(0, W1_PARTS[0])
+        gather_words(*WORD_PIECES[0])
+        round_weight(nc.vector.tensor_copy, 0, W1_PARTS[2])
+        quantize_weight(0, slice(W1_PARTS[1].start, N))
+        for piece in WORD_PIECES[1:]:
+            gather_words(*piece)
+
+        round_weight(nc.scalar.copy, 1, W2_PARTS[0])
+        round_weight(nc.vector.tensor_copy, 1, W2_PARTS[1])
+        quantize_weight(1, slice(0, N))
+        round_weight(nc.vector.tensor_copy, 2, slice(0, N))
+        quantize_weight(2, slice(0, N))
 
         accs = [psum.tile([P, N], F32, name=f"acc{b}") for b in range(ACC_BANKS)]
         turns = [psum.tile([P, PACK, P], F32, name=f"turn{b}") for b in range(TURN_BANKS)]
@@ -210,6 +218,6 @@ def tile_picked_zsmoe_gelu_po_kernel(tc, x_words, x_scales, w1, w2, w3, gate, of
                 if n == mix_at[group[-1]] + PACK_LAG:
                     pack(group)
 
-        for q in range(QUADRANTS):
-            queue = (nc.sync, nc.scalar)[q % 2]
-            queue.dma_start(out_2[0, 4 * q:4 * q + 4, :].bitcast(I32), y_scales[32 * q:32 * q + 4, :].bitcast(I32))
+        for r in range(4):
+            queue = (nc.sync, nc.scalar)[r % 2]
+            queue.dma_start(out_2[0, r:16:4, :].bitcast(I32), y_scales[r:P:32, :].bitcast(I32))

@@ -24,19 +24,33 @@ GELU = mybir.ActivationFunctionType.Gelu_apprx_tanh
 MULT = mybir.AluOpType.mult
 ADD = mybir.AluOpType.add
 
-W1_PARTS = (slice(0, 256), slice(256, 384), slice(384, N))
-W2_PARTS = (slice(0, 128), slice(128, N))
+HALF = N // 2
+W1_SCALAR = 384
+W2_POOL = 256
+W3_POOL = 128
+TIE3 = 1
+GATE_UNIT_A = 8
+GATE_UNIT_B = 12
+AHEAD = 3
+STAGGER = 2
+TURN_LATE = 1
 GATE_ROWS = slice(4, 4 * (D + 1), 4)
 WORD_PIECES = ((0, 256), (256, 256), (512, 512))
 GATE_PIECE = PACK * P
 ACC_BANKS = 4
 TURN_BANKS = 8 - ACC_BANKS
-SECOND_LAYER_LEAD = 6
+SECOND_LAYER_LEAD = 0
 VECTOR_SUM_FROM = 3
-MIX_LAG = 2
-PACK_LAG = 3
+MIX_LAG = 1
+FIRST_MIX = 10
+DRAIN_LAG = 2
+PACK_LAG = 2
 PAIR = 2
 GROUPS = ((0, 1), (2, 3), (4, 5), (6,), (7,))
+SCALAR_PACKS = (7,)
+VECTOR_DRAINS = ()
+EARLY_GATE = 2
+W3_AT = 8
 
 
 def interleave(copy, dst, src):
@@ -74,14 +88,21 @@ def tile_picked_zsmoe_gelu_po_kernel(tc, x_words, x_scales, w1, w2, w3, gate, of
         for r in range(4):
             nc.sync.dma_start(scale_window[r:P:32, :].bitcast(I32), x_scales[0, r:16:4, :].bitcast(I32))
         load_weight(0, slice(1, PACK))
+        if EARLY_GATE == 1:
+            nc.sync.dma_start(gate_window[GATE_ROWS, :], gate[:, 0, :])
         nc.sync.dma_start(word_window[:].bitcast(I32), x_words[0].rearrange("p n t -> p (n t)").bitcast(I32))
+        if EARLY_GATE == 2:
+            nc.sync.dma_start(gate_window[GATE_ROWS, :], gate[:, 0, :])
         load_weight(1, slice(0, PACK))
+        if EARLY_GATE == 3:
+            nc.sync.dma_start(gate_window[GATE_ROWS, :], gate[:, 0, :])
         load_weight(2, slice(0, PACK))
-        nc.sync.dma_start(gate_window[GATE_ROWS, :], gate[:, 0, :])
+        if EARLY_GATE == 0:
+            nc.sync.dma_start(gate_window[GATE_ROWS, :], gate[:, 0, :])
 
         nc.scalar.activation(warm[:, 1:2], warm[:, 0:1], GELU)
 
-        w_bf = [keep.tile([P, PACK * N], BF16, name=f"w_bf{d}", align_bytes=64) for d in range(D)]
+        w_bf = [keep.tile([P, PACK * N], BF16, name=f"w_bf{d}", align_bytes=64) for d in range(D - 1)]
         w_codes = [keep.tile([P, N], U32, name=f"w_codes{d}", align_bytes=64) for d in range(D)]
         w_scales = [keep.tile([P, N], U8, name=f"w_scales{d}", align_bytes=64) for d in range(D)]
 
@@ -95,11 +116,23 @@ def tile_picked_zsmoe_gelu_po_kernel(tc, x_words, x_scales, w1, w2, w3, gate, of
         def entries(first, count):
             return offsets[:, first // LIST_ROWS:(first + count) // LIST_ROWS]
 
-        def round_weight(copy, d, cols):
-            interleave(copy, w_bf[d][:, PACK * cols.start:PACK * cols.stop], w_raw[d][:, :, cols])
+        def round_weight(copy, d, first, last):
+            if last > first:
+                interleave(copy, w_bf[d][:, PACK * first:PACK * last], w_raw[d][:, :, first:last])
 
-        for cols in W1_PARTS[:2]:
-            round_weight(nc.scalar.copy, 0, cols)
+        def round_on_pool(d, last):
+            if last:
+                nc.gpsimd.tensor_scalar(
+                    w_bf[d][:, :PACK * last].rearrange("p (c t) -> p c t", t=PACK),
+                    w_raw[d][:, :, :last].rearrange("p t c -> p c t"),
+                    1.0,
+                    0.0,
+                    MULT,
+                    ADD,
+                )
+
+        round_weight(nc.scalar.copy, 0, 0, HALF)
+        round_weight(nc.scalar.copy, 0, HALF, W1_SCALAR)
 
         token_scales = keep.tile([P, S], U8, name="token_scales", align_bytes=64)
         nc.vector.tensor_copy(token_scales[:], scale_window[:].indirect(offsets[:]))
@@ -108,35 +141,42 @@ def tile_picked_zsmoe_gelu_po_kernel(tc, x_words, x_scales, w1, w2, w3, gate, of
         def gather_words(first, count):
             nc.vector.tensor_copy(token_words[:, first:first + count], word_window[:].indirect(entries(first, count)))
 
-        quantize_weight(0, W1_PARTS[0])
+        banks = [psum.tile([P, N], F32, name=f"bank{b}") for b in range(8)]
+        turns = [bank[:].rearrange("p (t m) -> p t m", t=PACK) for bank in banks[ACC_BANKS:]]
+        gates = keep.tile([P, TILES, D], F32, name="gates")
+        gate_pieces = S // GATE_PIECE
+
+        def gather_gates(u, tag):
+            gate_rows = keep.tile([P, GATE_PIECE], F32, name=f"gate_rows{u}", tag=tag, align_bytes=64)
+            nc.vector.tensor_copy(gate_rows[:], gate_window[:].indirect(entries(u * GATE_PIECE, GATE_PIECE)))
+            return gate_rows
+
+        def turn_gates(u, gate_rows):
+            bank = turns[TURN_BANKS - gate_pieces + u]
+            for a in range(PACK):
+                nc.tensor.transpose(bank[:, a, :], gate_rows[:, a * P:(a + 1) * P], ident[:])
+            nc.vector.tensor_copy(gates[:, PACK * u:PACK * (u + 1), :], bank[:, :, GATE_ROWS])
+
+        quantize_weight(0, slice(0, HALF))
         gather_words(*WORD_PIECES[0])
-        round_weight(nc.vector.tensor_copy, 0, W1_PARTS[2])
-        quantize_weight(0, slice(W1_PARTS[1].start, N))
+        round_weight(nc.vector.tensor_copy, 0, W1_SCALAR, N)
+        quantize_weight(0, slice(HALF, N))
         for piece in WORD_PIECES[1:]:
             gather_words(*piece)
 
-        round_weight(nc.scalar.copy, 1, W2_PARTS[0])
-        round_weight(nc.vector.tensor_copy, 1, W2_PARTS[1])
-        quantize_weight(1, slice(0, N))
-        round_weight(nc.vector.tensor_copy, 2, slice(0, N))
-        quantize_weight(2, slice(0, N))
-
-        accs = [psum.tile([P, N], F32, name=f"acc{b}") for b in range(ACC_BANKS)]
-        turns = [psum.tile([P, PACK, P], F32, name=f"turn{b}") for b in range(TURN_BANKS)]
-
-        gate_rows = keep.tile([P, S], F32, name="gate_rows", align_bytes=64)
-        gates = keep.tile([P, TILES, D], F32, name="gates")
-        gate_pieces = S // GATE_PIECE
-        for u in range(gate_pieces):
-            nc.vector.tensor_copy(
-                gate_rows[:, u * GATE_PIECE:(u + 1) * GATE_PIECE],
-                gate_window[:].indirect(entries(u * GATE_PIECE, GATE_PIECE)),
-            )
-        for u in range(gate_pieces):
-            for a in range(PACK):
-                i = PACK * u + a
-                nc.tensor.transpose(turns[u][:, a, :], gate_rows[:, i * P:(i + 1) * P], ident[:])
-            nc.vector.tensor_copy(gates[:, PACK * u:PACK * (u + 1), :], turns[u][:, :, GATE_ROWS])
+        rows = [gather_gates(0, "gate_rows0")]
+        round_on_pool(1, W2_POOL)
+        round_weight(nc.vector.tensor_copy, 1, W2_POOL, max(W2_POOL, HALF))
+        round_weight(nc.vector.tensor_copy, 1, max(W2_POOL, HALF), N)
+        quantize_weight(1, slice(HALF, N))
+        quantize_weight(1, slice(0, HALF))
+        rows.append(gather_gates(1, "w_raw1"))
+        w_bf.append(keep.tile([P, PACK * N], BF16, name="w_bf2", tag="w_bf1" if TIE3 else "w_bf2", align_bytes=64))
+        round_on_pool(2, W3_POOL)
+        round_weight(nc.vector.tensor_copy, 2, HALF, N)
+        round_weight(nc.vector.tensor_copy, 2, W3_POOL, HALF)
+        quantize_weight(2, slice(HALF, N))
+        quantize_weight(2, slice(0, HALF))
 
         y_codes = keep.tile([P, S], U32, name="y_codes", align_bytes=64)
         y_scales = keep.tile([P, S], U8, name="y_scales", align_bytes=64)
@@ -144,16 +184,22 @@ def tile_picked_zsmoe_gelu_po_kernel(tc, x_words, x_scales, w1, w2, w3, gate, of
         out_words = out_1[0].rearrange("p n t -> p (n t)").bitcast(I32)
 
         early = [(i, 0) for i in range(TILES)] + [(i, 1) for i in range(SECOND_LAYER_LEAD)]
-        units = early + [(i, d) for i in range(TILES) for d in range(D) if (i, d) not in early]
+        units = list(early)
+        for j in range(TILES + STAGGER):
+            units.extend(u for u in ((j, 1), (j - STAGGER, 2)) if u not in early and 0 <= u[0] < TILES)
         acts = {}
+        gated = {}
         ys = [keep.tile([P, PACK, PAIR * P], F32, name=f"y{pair}") for pair in range(TILES // PAIR)]
 
-        def turn_bank(i):
-            return turns[(gate_pieces + i) % TURN_BANKS]
+        gate_units = (GATE_UNIT_A, GATE_UNIT_B)
+        plain = [n for n in range(len(units)) if n not in gate_units]
 
-        def product(n):
+        def bank_of(n):
+            return banks[8 - gate_pieces + gate_units.index(n) if n in gate_units else plain.index(n) % ACC_BANKS]
+
+        def multiply(n):
             i, d = units[n]
-            acc = accs[n % ACC_BANKS]
+            acc = bank_of(n)
             nc.tensor.matmul_mx(
                 out=acc[:],
                 lhsT=token_words[:, i * P:(i + 1) * P].bitcast(FP8X4),
@@ -163,33 +209,37 @@ def tile_picked_zsmoe_gelu_po_kernel(tc, x_words, x_scales, w1, w2, w3, gate, of
                 start=True,
                 stop=True,
             )
+
+        def activate(n):
+            i, d = units[n]
+            acc = bank_of(n)
             acts[i, d] = keep.tile([P, PACK, P], F32, name=f"act{i}{d}")
             nc.scalar.activation(acts[i, d][:], acc[:].rearrange("p (m t) -> p t m", t=PACK), GELU)
 
-        def mix(i):
+        def weigh(i, d):
+            gated[i, d] = keep.tile([P, PACK * P], F32, name=f"gated{i}{d}")
+            act = acts[i, d][:].rearrange("p t m -> p (t m)")
+            if d == 1 and i >= VECTOR_SUM_FROM:
+                nc.vector.scalar_tensor_tensor(gated[i, d][:], act, gates[:, i, d:d + 1], gated[i, 0][:], MULT, ADD)
+            else:
+                nc.vector.tensor_scalar(gated[i, d][:], act, gates[:, i, d:d + 1], None, MULT)
+
+        def turn(i, d):
             first_turned = 1 if i >= VECTOR_SUM_FROM else 0
-            gated = []
-            for d in range(D):
-                gated.append(keep.tile([P, PACK * P], F32, name=f"gated{i}{d}"))
-                act = acts[i, d][:].rearrange("p t m -> p (t m)")
-                if d == first_turned == 1:
-                    nc.vector.scalar_tensor_tensor(gated[d][:], act, gates[:, i, d:d + 1], gated[0][:], MULT, ADD)
-                else:
-                    nc.vector.tensor_scalar(gated[d][:], act, gates[:, i, d:d + 1], None, MULT)
-                if d >= first_turned:
-                    for t in range(PACK):
-                        nc.tensor.matmul(
-                            turn_bank(i)[:, t, :],
-                            gated[d][:, t * P:(t + 1) * P],
-                            ident[:],
-                            is_transpose=True,
-                            start=(d == first_turned and t == 0),
-                            stop=(d == D - 1 and t == PACK - 1),
-                        )
+            for t in range(PACK * (d >= first_turned)):
+                nc.tensor.matmul(
+                    turns[i % TURN_BANKS][:, t, :],
+                    gated[i, d][:, t * P:(t + 1) * P],
+                    ident[:],
+                    is_transpose=True,
+                    start=(d == first_turned and t == 0),
+                    stop=(d == D - 1 and t == PACK - 1),
+                )
 
         def drain(i):
             pair, place = divmod(i, PAIR)
-            nc.scalar.copy(ys[pair][:, :, place * P:(place + 1) * P], turn_bank(i)[:])
+            copy = nc.vector.tensor_copy if i in VECTOR_DRAINS else nc.scalar.copy
+            copy(ys[pair][:, :, place * P:(place + 1) * P], turns[i % TURN_BANKS])
             if place == PAIR - 1:
                 nc.sync.dma_start(out_rows[:, :, pair * PAIR * P:(i + 1) * P], ys[pair][:])
 
@@ -198,25 +248,38 @@ def tile_picked_zsmoe_gelu_po_kernel(tc, x_words, x_scales, w1, w2, w3, gate, of
             pair, place = divmod(group[0], PAIR)
             y = ys[pair][:, :, place * P:(place + len(group)) * P]
             y_bf = keep.tile([P, PACK * P * len(group)], BF16, name=f"y_bf{group[0]}", align_bytes=64)
-            interleave(nc.scalar.copy if group == GROUPS[-1] else nc.vector.tensor_copy, y_bf[:], y)
+            interleave(nc.scalar.copy if group[0] in SCALAR_PACKS else nc.vector.tensor_copy, y_bf[:], y)
             nc.vector.quantize_mx(out=y_codes[:, cols].bitcast(FP8X4), scales=y_scales[:, cols], in_=y_bf[:])
             if group != GROUPS[-2]:
                 first = GROUPS[-2][0] * P if group == GROUPS[-1] else cols.start
                 nc.sync.dma_start(out_words[:, first:cols.stop], y_codes[:, first:cols.stop].bitcast(I32))
 
-        mix_at = []
-        for i in range(TILES):
-            mix_at.append(max([units.index((i, D - 1))] + mix_at[-1:]) + MIX_LAG)
-        for n in range(mix_at[-1] + PACK_LAG + 1):
+        weighed, turned, drained, packed = {}, {}, {}, {}
+        for n in range(AHEAD + 1):
+            multiply(n)
+        for n in range(len(units) + MIX_LAG + DRAIN_LAG + PACK_LAG + TILES):
             if n < len(units):
-                product(n)
-            if n in mix_at:
-                mix(mix_at.index(n))
-            if n - 1 in mix_at:
-                drain(mix_at.index(n - 1))
+                activate(n)
+            if n + AHEAD + 1 < len(units):
+                multiply(n + AHEAD + 1)
+            if n in gate_units:
+                turn_gates(gate_units.index(n), rows[gate_units.index(n)])
+            for i in range(TILES):
+                if (i, D - 1) in turned and i not in drained and n >= turned[i, D - 1] + DRAIN_LAG:
+                    drain(i)
+                    drained[i] = n
+            for m, (i, d) in enumerate(units):
+                bank_free = i < TURN_BANKS or i - TURN_BANKS in drained
+                if (i, d) not in weighed and n >= max(m + MIX_LAG, FIRST_MIX, GATE_UNIT_B) and bank_free:
+                    weigh(i, d)
+                    for e in range(D) if TURN_LATE else (d,):
+                        if d == D - 1 or not TURN_LATE:
+                            turn(i, e)
+                    weighed[i, d] = turned[i, d] = n
             for group in GROUPS:
-                if n == mix_at[group[-1]] + PACK_LAG:
+                if group not in packed and group[-1] in drained and n >= drained[group[-1]] + PACK_LAG:
                     pack(group)
+                    packed[group] = n
 
         for r in range(4):
             queue = (nc.sync, nc.scalar)[r % 2]

@@ -26,22 +26,25 @@ ADD = mybir.AluOpType.add
 
 HALF = N // 2
 W1_SCALAR = 384
-W2_POOL = 256
-W3_POOL = 128
+A_FIRST = 1
+B_AT = 8
+WORD_STORES = (1, 3, 5, 7)
+OUT_STORES = (1, 3, 5, 7)
+W3_POOL = 0
 TIE3 = 1
-GATE_UNIT_A = 8
+GATE_UNIT_A = 4
 GATE_UNIT_B = 12
 AHEAD = 3
-STAGGER = 2
-TURN_LATE = 1
+STAGGER = 4
+TURN_LATE = 0
 GATE_ROWS = slice(4, 4 * (D + 1), 4)
 WORD_PIECES = ((0, 256), (256, 256), (512, 512))
 GATE_PIECE = PACK * P
 ACC_BANKS = 4
 TURN_BANKS = 8 - ACC_BANKS
 SECOND_LAYER_LEAD = 0
-VECTOR_SUM_FROM = 3
-MIX_LAG = 1
+VECTOR_SUM_FROM = 4
+MIX_LAG = 0
 FIRST_MIX = 10
 DRAIN_LAG = 2
 PACK_LAG = 2
@@ -50,7 +53,7 @@ GROUPS = ((0, 1), (2, 3), (4, 5), (6,), (7,))
 SCALAR_PACKS = (7,)
 VECTOR_DRAINS = ()
 EARLY_GATE = 2
-W3_AT = 8
+W3_AT = 6
 
 
 def interleave(copy, dst, src):
@@ -120,17 +123,6 @@ def tile_picked_zsmoe_gelu_po_kernel(tc, x_words, x_scales, w1, w2, w3, gate, of
             if last > first:
                 interleave(copy, w_bf[d][:, PACK * first:PACK * last], w_raw[d][:, :, first:last])
 
-        def round_on_pool(d, last):
-            if last:
-                nc.gpsimd.tensor_scalar(
-                    w_bf[d][:, :PACK * last].rearrange("p (c t) -> p c t", t=PACK),
-                    w_raw[d][:, :, :last].rearrange("p t c -> p c t"),
-                    1.0,
-                    0.0,
-                    MULT,
-                    ADD,
-                )
-
         round_weight(nc.scalar.copy, 0, 0, HALF)
         round_weight(nc.scalar.copy, 0, HALF, W1_SCALAR)
 
@@ -143,7 +135,7 @@ def tile_picked_zsmoe_gelu_po_kernel(tc, x_words, x_scales, w1, w2, w3, gate, of
 
         banks = [psum.tile([P, N], F32, name=f"bank{b}") for b in range(8)]
         turns = [bank[:].rearrange("p (t m) -> p t m", t=PACK) for bank in banks[ACC_BANKS:]]
-        gates = keep.tile([P, TILES, D], F32, name="gates")
+        gates = {}
         gate_pieces = S // GATE_PIECE
 
         def gather_gates(u, tag):
@@ -155,7 +147,8 @@ def tile_picked_zsmoe_gelu_po_kernel(tc, x_words, x_scales, w1, w2, w3, gate, of
             bank = turns[TURN_BANKS - gate_pieces + u]
             for a in range(PACK):
                 nc.tensor.transpose(bank[:, a, :], gate_rows[:, a * P:(a + 1) * P], ident[:])
-            nc.vector.tensor_copy(gates[:, PACK * u:PACK * (u + 1), :], bank[:, :, GATE_ROWS])
+            gates[u] = keep.tile([P, PACK, D], F32, name=f"gates{u}", tag=("w_raw1", "gates1")[u], align_bytes=64)
+            nc.vector.tensor_copy(gates[u][:], bank[:, :, GATE_ROWS])
 
         quantize_weight(0, slice(0, HALF))
         gather_words(*WORD_PIECES[0])
@@ -164,19 +157,21 @@ def tile_picked_zsmoe_gelu_po_kernel(tc, x_words, x_scales, w1, w2, w3, gate, of
         for piece in WORD_PIECES[1:]:
             gather_words(*piece)
 
-        rows = [gather_gates(0, "gate_rows0")]
-        round_on_pool(1, W2_POOL)
-        round_weight(nc.vector.tensor_copy, 1, W2_POOL, max(W2_POOL, HALF))
-        round_weight(nc.vector.tensor_copy, 1, max(W2_POOL, HALF), N)
-        quantize_weight(1, slice(HALF, N))
-        quantize_weight(1, slice(0, HALF))
-        rows.append(gather_gates(1, "w_raw1"))
+        def prepare_weight(d):
+            for first in (0, HALF):
+                round_weight(nc.vector.tensor_copy, d, first, first + HALF)
+            for first in (0, HALF):
+                quantize_weight(d, slice(first, first + HALF))
+
+        rows = {}
+        if A_FIRST:
+            rows[0] = gather_gates(0, "gate_rows0")
+        prepare_weight(1)
+        if not A_FIRST:
+            rows[0] = gather_gates(0, "w_raw1")
+        if B_AT < 0:
+            rows[1] = gather_gates(1, "w_raw1" if A_FIRST else "gate_rows1")
         w_bf.append(keep.tile([P, PACK * N], BF16, name="w_bf2", tag="w_bf1" if TIE3 else "w_bf2", align_bytes=64))
-        round_on_pool(2, W3_POOL)
-        round_weight(nc.vector.tensor_copy, 2, HALF, N)
-        round_weight(nc.vector.tensor_copy, 2, W3_POOL, HALF)
-        quantize_weight(2, slice(HALF, N))
-        quantize_weight(2, slice(0, HALF))
 
         y_codes = keep.tile([P, S], U32, name="y_codes", align_bytes=64)
         y_scales = keep.tile([P, S], U8, name="y_scales", align_bytes=64)
@@ -220,9 +215,9 @@ def tile_picked_zsmoe_gelu_po_kernel(tc, x_words, x_scales, w1, w2, w3, gate, of
             gated[i, d] = keep.tile([P, PACK * P], F32, name=f"gated{i}{d}")
             act = acts[i, d][:].rearrange("p t m -> p (t m)")
             if d == 1 and i >= VECTOR_SUM_FROM:
-                nc.vector.scalar_tensor_tensor(gated[i, d][:], act, gates[:, i, d:d + 1], gated[i, 0][:], MULT, ADD)
+                nc.vector.scalar_tensor_tensor(gated[i, d][:], act, gates[i // PACK][:, i % PACK, d:d + 1], gated[i, 0][:], MULT, ADD)
             else:
-                nc.vector.tensor_scalar(gated[i, d][:], act, gates[:, i, d:d + 1], None, MULT)
+                nc.vector.tensor_scalar(gated[i, d][:], act, gates[i // PACK][:, i % PACK, d:d + 1], None, MULT)
 
         def turn(i, d):
             first_turned = 1 if i >= VECTOR_SUM_FROM else 0
@@ -240,8 +235,11 @@ def tile_picked_zsmoe_gelu_po_kernel(tc, x_words, x_scales, w1, w2, w3, gate, of
             pair, place = divmod(i, PAIR)
             copy = nc.vector.tensor_copy if i in VECTOR_DRAINS else nc.scalar.copy
             copy(ys[pair][:, :, place * P:(place + 1) * P], turns[i % TURN_BANKS])
-            if place == PAIR - 1:
-                nc.sync.dma_start(out_rows[:, :, pair * PAIR * P:(i + 1) * P], ys[pair][:])
+            if i in OUT_STORES:
+                first = 0 if i - 1 not in OUT_STORES else place
+                nc.sync.dma_start(
+                    out_rows[:, :, (pair * PAIR + first) * P:(i + 1) * P], ys[pair][:, :, first * P:(place + 1) * P]
+                )
 
         def pack(group):
             cols = slice(group[0] * P, (group[-1] + 1) * P)
@@ -250,18 +248,22 @@ def tile_picked_zsmoe_gelu_po_kernel(tc, x_words, x_scales, w1, w2, w3, gate, of
             y_bf = keep.tile([P, PACK * P * len(group)], BF16, name=f"y_bf{group[0]}", align_bytes=64)
             interleave(nc.scalar.copy if group[0] in SCALAR_PACKS else nc.vector.tensor_copy, y_bf[:], y)
             nc.vector.quantize_mx(out=y_codes[:, cols].bitcast(FP8X4), scales=y_scales[:, cols], in_=y_bf[:])
-            if group != GROUPS[-2]:
-                first = GROUPS[-2][0] * P if group == GROUPS[-1] else cols.start
+            if group[-1] in WORD_STORES:
+                first = (max([-1] + [i for i in WORD_STORES if i < group[-1]]) + 1) * P
                 nc.sync.dma_start(out_words[:, first:cols.stop], y_codes[:, first:cols.stop].bitcast(I32))
 
         weighed, turned, drained, packed = {}, {}, {}, {}
         for n in range(AHEAD + 1):
             multiply(n)
         for n in range(len(units) + MIX_LAG + DRAIN_LAG + PACK_LAG + TILES):
+            if n == W3_AT:
+                prepare_weight(2)
             if n < len(units):
                 activate(n)
             if n + AHEAD + 1 < len(units):
                 multiply(n + AHEAD + 1)
+            if n == B_AT:
+                rows[1] = gather_gates(1, "w_raw2")
             if n in gate_units:
                 turn_gates(gate_units.index(n), rows[gate_units.index(n)])
             for i in range(TILES):
@@ -270,10 +272,11 @@ def tile_picked_zsmoe_gelu_po_kernel(tc, x_words, x_scales, w1, w2, w3, gate, of
                     drained[i] = n
             for m, (i, d) in enumerate(units):
                 bank_free = i < TURN_BANKS or i - TURN_BANKS in drained
-                if (i, d) not in weighed and n >= max(m + MIX_LAG, FIRST_MIX, GATE_UNIT_B) and bank_free:
+                if (i, d) not in weighed and n >= max(m + MIX_LAG, gate_units[i // PACK]) and bank_free:
                     weigh(i, d)
-                    for e in range(D) if TURN_LATE else (d,):
-                        if d == D - 1 or not TURN_LATE:
+                    late = i >= TURN_LATE
+                    for e in range(D) if late else (d,):
+                        if d == D - 1 or not late:
                             turn(i, e)
                     weighed[i, d] = turned[i, d] = n
             for group in GROUPS:

@@ -6,7 +6,8 @@ from concourse.masks import make_identity
 K, T, S, D, N = 512, 2048, 1024, 3, 512
 P = 128
 PACK = 4
-QUADRANTS = 4
+QUADRANT = 32
+SCALE_ROWS = 4
 LIST_ROWS = 16
 TILES = S // P
 
@@ -26,34 +27,19 @@ ADD = mybir.AluOpType.add
 
 HALF = N // 2
 W1_SCALAR = 384
-A_FIRST = 1
-B_AT = 8
-WORD_STORES = (1, 3, 5, 7)
-OUT_STORES = (1, 3, 5, 7)
-W3_POOL = 0
-TIE3 = 1
-GATE_UNIT_A = 4
-GATE_UNIT_B = 12
-AHEAD = 3
-STAGGER = 4
-TURN_LATE = 0
 GATE_ROWS = slice(4, 4 * (D + 1), 4)
 WORD_PIECES = ((0, 256), (256, 256), (512, 512))
-GATE_PIECE = PACK * P
-ACC_BANKS = 4
-TURN_BANKS = 8 - ACC_BANKS
-SECOND_LAYER_LEAD = 0
+GATE_TILES = 4
+BANKS = 8
+PRODUCT_BANKS = 4
+TURN_BANKS = BANKS - PRODUCT_BANKS
+GATE_UNITS = (3, 12)
+STAGGER = 4
 VECTOR_SUM_FROM = 4
-MIX_LAG = 0
-FIRST_MIX = 10
 DRAIN_LAG = 2
 PACK_LAG = 2
 PAIR = 2
 GROUPS = ((0, 1), (2, 3), (4, 5), (6,), (7,))
-SCALAR_PACKS = (7,)
-VECTOR_DRAINS = ()
-EARLY_GATE = 2
-W3_AT = 6
 
 
 def interleave(copy, dst, src):
@@ -86,22 +72,17 @@ def tile_picked_zsmoe_gelu_po_kernel(tc, x_words, x_scales, w1, w2, w3, gate, of
         def load_weight(d, rows):
             nc.sync.dma_start(w_raw[d][:, rows, :], (w1, w2, w3)[d].rearrange("(p t) m -> p t m", t=PACK)[:, rows, :])
 
-        nc.sync.dma_start(offsets[:], offs)
         load_weight(0, slice(0, 1))
-        for r in range(4):
-            nc.sync.dma_start(scale_window[r:P:32, :].bitcast(I32), x_scales[0, r:16:4, :].bitcast(I32))
+        nc.sync.dma_start(offsets[:], offs)
+        for r in range(SCALE_ROWS):
+            nc.sync.dma_start(
+                scale_window[r:P:QUADRANT, :].bitcast(I32), x_scales[0, r:K // 32:SCALE_ROWS, :].bitcast(I32)
+            )
         load_weight(0, slice(1, PACK))
-        if EARLY_GATE == 1:
-            nc.sync.dma_start(gate_window[GATE_ROWS, :], gate[:, 0, :])
         nc.sync.dma_start(word_window[:].bitcast(I32), x_words[0].rearrange("p n t -> p (n t)").bitcast(I32))
-        if EARLY_GATE == 2:
-            nc.sync.dma_start(gate_window[GATE_ROWS, :], gate[:, 0, :])
+        nc.sync.dma_start(gate_window[GATE_ROWS, :], gate[:, 0, :])
         load_weight(1, slice(0, PACK))
-        if EARLY_GATE == 3:
-            nc.sync.dma_start(gate_window[GATE_ROWS, :], gate[:, 0, :])
         load_weight(2, slice(0, PACK))
-        if EARLY_GATE == 0:
-            nc.sync.dma_start(gate_window[GATE_ROWS, :], gate[:, 0, :])
 
         nc.scalar.activation(warm[:, 1:2], warm[:, 0:1], GELU)
 
@@ -109,19 +90,24 @@ def tile_picked_zsmoe_gelu_po_kernel(tc, x_words, x_scales, w1, w2, w3, gate, of
         w_codes = [keep.tile([P, N], U32, name=f"w_codes{d}", align_bytes=64) for d in range(D)]
         w_scales = [keep.tile([P, N], U8, name=f"w_scales{d}", align_bytes=64) for d in range(D)]
 
-        def quantize_weight(d, cols):
+        def round_weight(copy, d, first, last):
+            interleave(copy, w_bf[d][:, PACK * first:PACK * last], w_raw[d][:, :, first:last])
+
+        def quantize_weight(d, first):
             nc.vector.quantize_mx(
-                out=w_codes[d][:, cols].bitcast(FP8X4),
-                scales=w_scales[d][:, cols],
-                in_=w_bf[d][:, PACK * cols.start:PACK * cols.stop],
+                out=w_codes[d][:, first:first + HALF].bitcast(FP8X4),
+                scales=w_scales[d][:, first:first + HALF],
+                in_=w_bf[d][:, PACK * first:PACK * (first + HALF)],
             )
+
+        def prepare_weight(d):
+            for first in (0, HALF):
+                round_weight(nc.vector.tensor_copy, d, first, first + HALF)
+            for first in (0, HALF):
+                quantize_weight(d, first)
 
         def entries(first, count):
             return offsets[:, first // LIST_ROWS:(first + count) // LIST_ROWS]
-
-        def round_weight(copy, d, first, last):
-            if last > first:
-                interleave(copy, w_bf[d][:, PACK * first:PACK * last], w_raw[d][:, :, first:last])
 
         round_weight(nc.scalar.copy, 0, 0, HALF)
         round_weight(nc.scalar.copy, 0, HALF, W1_SCALAR)
@@ -133,70 +119,57 @@ def tile_picked_zsmoe_gelu_po_kernel(tc, x_words, x_scales, w1, w2, w3, gate, of
         def gather_words(first, count):
             nc.vector.tensor_copy(token_words[:, first:first + count], word_window[:].indirect(entries(first, count)))
 
-        banks = [psum.tile([P, N], F32, name=f"bank{b}") for b in range(8)]
-        turns = [bank[:].rearrange("p (t m) -> p t m", t=PACK) for bank in banks[ACC_BANKS:]]
-        gates = {}
-        gate_pieces = S // GATE_PIECE
-
-        def gather_gates(u, tag):
-            gate_rows = keep.tile([P, GATE_PIECE], F32, name=f"gate_rows{u}", tag=tag, align_bytes=64)
-            nc.vector.tensor_copy(gate_rows[:], gate_window[:].indirect(entries(u * GATE_PIECE, GATE_PIECE)))
-            return gate_rows
-
-        def turn_gates(u, gate_rows):
-            bank = turns[TURN_BANKS - gate_pieces + u]
-            for a in range(PACK):
-                nc.tensor.transpose(bank[:, a, :], gate_rows[:, a * P:(a + 1) * P], ident[:])
-            gates[u] = keep.tile([P, PACK, D], F32, name=f"gates{u}", tag=("w_raw1", "gates1")[u], align_bytes=64)
-            nc.vector.tensor_copy(gates[u][:], bank[:, :, GATE_ROWS])
-
-        quantize_weight(0, slice(0, HALF))
+        quantize_weight(0, 0)
         gather_words(*WORD_PIECES[0])
         round_weight(nc.vector.tensor_copy, 0, W1_SCALAR, N)
-        quantize_weight(0, slice(HALF, N))
+        quantize_weight(0, HALF)
         for piece in WORD_PIECES[1:]:
             gather_words(*piece)
 
-        def prepare_weight(d):
-            for first in (0, HALF):
-                round_weight(nc.vector.tensor_copy, d, first, first + HALF)
-            for first in (0, HALF):
-                quantize_weight(d, slice(first, first + HALF))
+        banks = [psum.tile([P, N], F32, name=f"bank{b}") for b in range(BANKS)]
+        turn_banks = [bank[:].rearrange("p (t j) -> p t j", t=PACK) for bank in banks[PRODUCT_BANKS:]]
+        gate_rows = []
+        gates = []
 
-        rows = {}
-        if A_FIRST:
-            rows[0] = gather_gates(0, "gate_rows0")
+        def gather_gates(tag):
+            u = len(gate_rows)
+            gate_rows.append(keep.tile([P, GATE_TILES * P], F32, name=f"gate_rows{u}", tag=tag, align_bytes=64))
+            nc.vector.tensor_copy(gate_rows[u][:], gate_window[:].indirect(entries(u * GATE_TILES * P, GATE_TILES * P)))
+
+        def gate_bank(u):
+            return BANKS - len(GATE_UNITS) + u
+
+        def turn_gates(u, tag):
+            bank = turn_banks[gate_bank(u) - PRODUCT_BANKS]
+            for a in range(GATE_TILES):
+                nc.tensor.transpose(bank[:, a, :], gate_rows[u][:, a * P:(a + 1) * P], ident[:])
+            gates.append(keep.tile([P, GATE_TILES, D], F32, name=f"gates{u}", tag=tag, align_bytes=64))
+            nc.vector.tensor_copy(gates[u][:], bank[:, :, GATE_ROWS])
+
+        gather_gates("gate_rows0")
         prepare_weight(1)
-        if not A_FIRST:
-            rows[0] = gather_gates(0, "w_raw1")
-        if B_AT < 0:
-            rows[1] = gather_gates(1, "w_raw1" if A_FIRST else "gate_rows1")
-        w_bf.append(keep.tile([P, PACK * N], BF16, name="w_bf2", tag="w_bf1" if TIE3 else "w_bf2", align_bytes=64))
+        w_bf.append(keep.tile([P, PACK * N], BF16, name="w_bf2", tag="w_bf1", align_bytes=64))
 
         y_codes = keep.tile([P, S], U32, name="y_codes", align_bytes=64)
         y_scales = keep.tile([P, S], U8, name="y_scales", align_bytes=64)
         out_rows = out_0.rearrange("(p t) j -> p t j", t=PACK)
         out_words = out_1[0].rearrange("p n t -> p (n t)").bitcast(I32)
 
-        early = [(i, 0) for i in range(TILES)] + [(i, 1) for i in range(SECOND_LAYER_LEAD)]
-        units = list(early)
+        units = [(i, 0) for i in range(TILES)]
         for j in range(TILES + STAGGER):
-            units.extend(u for u in ((j, 1), (j - STAGGER, 2)) if u not in early and 0 <= u[0] < TILES)
+            units.extend(unit for unit in ((j, 1), (j - STAGGER, 2)) if 0 <= unit[0] < TILES)
+        rotating = [n for n in range(len(units)) if n not in GATE_UNITS]
         acts = {}
         gated = {}
         ys = [keep.tile([P, PACK, PAIR * P], F32, name=f"y{pair}") for pair in range(TILES // PAIR)]
 
-        gate_units = (GATE_UNIT_A, GATE_UNIT_B)
-        plain = [n for n in range(len(units)) if n not in gate_units]
-
-        def bank_of(n):
-            return banks[8 - gate_pieces + gate_units.index(n) if n in gate_units else plain.index(n) % ACC_BANKS]
+        def product_bank(n):
+            return banks[gate_bank(GATE_UNITS.index(n)) if n in GATE_UNITS else rotating.index(n) % PRODUCT_BANKS]
 
         def multiply(n):
             i, d = units[n]
-            acc = bank_of(n)
             nc.tensor.matmul_mx(
-                out=acc[:],
+                out=product_bank(n)[:],
                 lhsT=token_words[:, i * P:(i + 1) * P].bitcast(FP8X4),
                 lhsT_scale=token_scales[:, i * P:(i + 1) * P],
                 rhs=w_codes[d][:].bitcast(FP8X4),
@@ -206,84 +179,80 @@ def tile_picked_zsmoe_gelu_po_kernel(tc, x_words, x_scales, w1, w2, w3, gate, of
             )
 
         def activate(n):
-            i, d = units[n]
-            acc = bank_of(n)
-            acts[i, d] = keep.tile([P, PACK, P], F32, name=f"act{i}{d}")
-            nc.scalar.activation(acts[i, d][:], acc[:].rearrange("p (m t) -> p t m", t=PACK), GELU)
+            acts[units[n]] = keep.tile([P, PACK, P], F32, name=f"act{n}")
+            nc.scalar.activation(acts[units[n]][:], product_bank(n)[:].rearrange("p (m t) -> p t m", t=PACK), GELU)
 
         def weigh(i, d):
             gated[i, d] = keep.tile([P, PACK * P], F32, name=f"gated{i}{d}")
             act = acts[i, d][:].rearrange("p t m -> p (t m)")
+            factor = gates[i // GATE_TILES][:, i % GATE_TILES, d:d + 1]
             if d == 1 and i >= VECTOR_SUM_FROM:
-                nc.vector.scalar_tensor_tensor(gated[i, d][:], act, gates[i // PACK][:, i % PACK, d:d + 1], gated[i, 0][:], MULT, ADD)
+                nc.vector.scalar_tensor_tensor(gated[i, d][:], act, factor, gated[i, 0][:], MULT, ADD)
             else:
-                nc.vector.tensor_scalar(gated[i, d][:], act, gates[i // PACK][:, i % PACK, d:d + 1], None, MULT)
+                nc.vector.tensor_scalar(gated[i, d][:], act, factor, None, MULT)
 
-        def turn(i, d):
-            first_turned = 1 if i >= VECTOR_SUM_FROM else 0
-            for t in range(PACK * (d >= first_turned)):
-                nc.tensor.matmul(
-                    turns[i % TURN_BANKS][:, t, :],
-                    gated[i, d][:, t * P:(t + 1) * P],
-                    ident[:],
-                    is_transpose=True,
-                    start=(d == first_turned and t == 0),
-                    stop=(d == D - 1 and t == PACK - 1),
-                )
+        def turn(i):
+            first_layer = 1 if i >= VECTOR_SUM_FROM else 0
+            for d in range(first_layer, D):
+                for t in range(PACK):
+                    nc.tensor.matmul(
+                        turn_banks[i % TURN_BANKS][:, t, :],
+                        gated[i, d][:, t * P:(t + 1) * P],
+                        ident[:],
+                        is_transpose=True,
+                        start=(d == first_layer and t == 0),
+                        stop=(d == D - 1 and t == PACK - 1),
+                    )
 
         def drain(i):
             pair, place = divmod(i, PAIR)
-            copy = nc.vector.tensor_copy if i in VECTOR_DRAINS else nc.scalar.copy
-            copy(ys[pair][:, :, place * P:(place + 1) * P], turns[i % TURN_BANKS])
-            if i in OUT_STORES:
-                first = 0 if i - 1 not in OUT_STORES else place
-                nc.sync.dma_start(
-                    out_rows[:, :, (pair * PAIR + first) * P:(i + 1) * P], ys[pair][:, :, first * P:(place + 1) * P]
-                )
+            nc.scalar.copy(ys[pair][:, :, place * P:(place + 1) * P], turn_banks[i % TURN_BANKS])
+            if place == PAIR - 1:
+                nc.sync.dma_start(out_rows[:, :, pair * PAIR * P:(i + 1) * P], ys[pair][:])
 
         def pack(group):
             cols = slice(group[0] * P, (group[-1] + 1) * P)
             pair, place = divmod(group[0], PAIR)
             y = ys[pair][:, :, place * P:(place + len(group)) * P]
             y_bf = keep.tile([P, PACK * P * len(group)], BF16, name=f"y_bf{group[0]}", align_bytes=64)
-            interleave(nc.scalar.copy if group[0] in SCALAR_PACKS else nc.vector.tensor_copy, y_bf[:], y)
+            interleave(nc.scalar.copy if group == GROUPS[-1] else nc.vector.tensor_copy, y_bf[:], y)
             nc.vector.quantize_mx(out=y_codes[:, cols].bitcast(FP8X4), scales=y_scales[:, cols], in_=y_bf[:])
-            if group[-1] in WORD_STORES:
-                first = (max([-1] + [i for i in WORD_STORES if i < group[-1]]) + 1) * P
-                nc.sync.dma_start(out_words[:, first:cols.stop], y_codes[:, first:cols.stop].bitcast(I32))
+            if group[-1] % PAIR == PAIR - 1:
+                pair_cols = slice(pair * PAIR * P, cols.stop)
+                nc.sync.dma_start(out_words[:, pair_cols], y_codes[:, pair_cols].bitcast(I32))
 
-        weighed, turned, drained, packed = {}, {}, {}, {}
-        for n in range(AHEAD + 1):
+        weighed, packed = set(), set()
+        turned, drained = {}, {}
+        for n in range(PRODUCT_BANKS):
             multiply(n)
-        for n in range(len(units) + MIX_LAG + DRAIN_LAG + PACK_LAG + TILES):
-            if n == W3_AT:
+        for n in range(len(units) + DRAIN_LAG + PACK_LAG):
+            if n == GATE_UNITS[0] + 1:
                 prepare_weight(2)
+                gather_gates("w_raw2")
             if n < len(units):
                 activate(n)
-            if n + AHEAD + 1 < len(units):
-                multiply(n + AHEAD + 1)
-            if n == B_AT:
-                rows[1] = gather_gates(1, "w_raw2")
-            if n in gate_units:
-                turn_gates(gate_units.index(n), rows[gate_units.index(n)])
-            for i in range(TILES):
-                if (i, D - 1) in turned and i not in drained and n >= turned[i, D - 1] + DRAIN_LAG:
+            if n + PRODUCT_BANKS < len(units):
+                multiply(n + PRODUCT_BANKS)
+            if n in GATE_UNITS:
+                turn_gates(GATE_UNITS.index(n), ("w_raw1", "gates1")[GATE_UNITS.index(n)])
+            for i in turned:
+                if i not in drained and n >= turned[i] + DRAIN_LAG:
                     drain(i)
                     drained[i] = n
-            for m, (i, d) in enumerate(units):
-                bank_free = i < TURN_BANKS or i - TURN_BANKS in drained
-                if (i, d) not in weighed and n >= max(m + MIX_LAG, gate_units[i // PACK]) and bank_free:
+            for i, d in units[:n + 1]:
+                if (i, d) not in weighed and i // GATE_TILES < len(gates) and (i < TURN_BANKS or i - TURN_BANKS in drained):
                     weigh(i, d)
-                    late = i >= TURN_LATE
-                    for e in range(D) if late else (d,):
-                        if d == D - 1 or not late:
-                            turn(i, e)
-                    weighed[i, d] = turned[i, d] = n
+                    weighed.add((i, d))
+                    if d == D - 1:
+                        turn(i)
+                        turned[i] = n
             for group in GROUPS:
                 if group not in packed and group[-1] in drained and n >= drained[group[-1]] + PACK_LAG:
                     pack(group)
-                    packed[group] = n
+                    packed.add(group)
 
-        for r in range(4):
+        for r in range(SCALE_ROWS):
             queue = (nc.sync, nc.scalar)[r % 2]
-            queue.dma_start(out_2[0, r:16:4, :].bitcast(I32), y_scales[r:P:32, :].bitcast(I32))
+            queue.dma_start(
+                out_2[0, r:N // 32:SCALE_ROWS, :].bitcast(I32), y_scales[r:P:QUADRANT, :].bitcast(I32)
+            )

@@ -27,6 +27,7 @@ ADD = mybir.AluOpType.add
 
 HALF = N // 2
 W1_SCALAR = 384
+W2_SCALAR = 128
 GATE_ROWS = slice(4, 4 * (D + 1), 4)
 WORD_PIECES = ((0, 256), (256, 256), (512, 512))
 GATE_TILES = 4
@@ -67,22 +68,22 @@ def tile_picked_zsmoe_gelu_po_kernel(tc, x_words, x_scales, w1, w2, w3, gate, of
         nc.vector.memset(gate_window[:], 0.0)
         make_identity(nc, ident[:])
 
+        w_rows = [w.rearrange("(p t) m -> p t m", t=PACK) for w in (w1, w2, w3)]
         w_raw = [keep.tile([P, PACK, N], F32, name=f"w_raw{d}", align_bytes=64) for d in range(D)]
+        w2_head = keep.tile([P, PACK, W2_SCALAR], F32, name="w2_head", align_bytes=64)
 
-        def load_weight(d, rows):
-            nc.sync.dma_start(w_raw[d][:, rows, :], (w1, w2, w3)[d].rearrange("(p t) m -> p t m", t=PACK)[:, rows, :])
-
-        load_weight(0, slice(0, 1))
+        nc.sync.dma_start(w_raw[0][:, :1, :], w_rows[0][:, :1, :])
         nc.sync.dma_start(offsets[:], offs)
         for r in range(SCALE_ROWS):
             nc.sync.dma_start(
                 scale_window[r:P:QUADRANT, :].bitcast(I32), x_scales[0, r:K // 32:SCALE_ROWS, :].bitcast(I32)
             )
-        load_weight(0, slice(1, PACK))
+        nc.sync.dma_start(w_raw[0][:, 1:, :], w_rows[0][:, 1:, :])
         nc.sync.dma_start(word_window[:].bitcast(I32), x_words[0].rearrange("p n t -> p (n t)").bitcast(I32))
+        nc.sync.dma_start(w2_head[:], w_rows[1][:, :, :W2_SCALAR])
         nc.sync.dma_start(gate_window[GATE_ROWS, :], gate[:, 0, :])
-        load_weight(1, slice(0, PACK))
-        load_weight(2, slice(0, PACK))
+        nc.sync.dma_start(w_raw[1][:, :, W2_SCALAR:], w_rows[1][:, :, W2_SCALAR:])
+        nc.sync.dma_start(w_raw[2][:], w_rows[2])
 
         nc.scalar.activation(warm[:, 1:2], warm[:, 0:1], GELU)
 
@@ -100,9 +101,9 @@ def tile_picked_zsmoe_gelu_po_kernel(tc, x_words, x_scales, w1, w2, w3, gate, of
                 in_=w_bf[d][:, PACK * first:PACK * (first + HALF)],
             )
 
-        def prepare_weight(d):
-            for first in (0, HALF):
-                round_weight(nc.vector.tensor_copy, d, first, first + HALF)
+        def prepare_weight(d, rounded):
+            round_weight(nc.vector.tensor_copy, d, rounded, HALF)
+            round_weight(nc.vector.tensor_copy, d, HALF, N)
             for first in (0, HALF):
                 quantize_weight(d, first)
 
@@ -111,6 +112,7 @@ def tile_picked_zsmoe_gelu_po_kernel(tc, x_words, x_scales, w1, w2, w3, gate, of
 
         round_weight(nc.scalar.copy, 0, 0, HALF)
         round_weight(nc.scalar.copy, 0, HALF, W1_SCALAR)
+        interleave(nc.scalar.copy, w_bf[1][:, :PACK * W2_SCALAR], w2_head[:])
 
         token_scales = keep.tile([P, S], U8, name="token_scales", align_bytes=64)
         nc.vector.tensor_copy(token_scales[:], scale_window[:].indirect(offsets[:]))
@@ -147,7 +149,7 @@ def tile_picked_zsmoe_gelu_po_kernel(tc, x_words, x_scales, w1, w2, w3, gate, of
             nc.vector.tensor_copy(gates[u][:], bank[:, :, GATE_ROWS])
 
         gather_gates("gate_rows0")
-        prepare_weight(1)
+        prepare_weight(1, W2_SCALAR)
         w_bf.append(keep.tile([P, PACK * N], BF16, name="w_bf2", tag="w_bf1", align_bytes=64))
 
         y_codes = keep.tile([P, S], U32, name="y_codes", align_bytes=64)
@@ -227,7 +229,7 @@ def tile_picked_zsmoe_gelu_po_kernel(tc, x_words, x_scales, w1, w2, w3, gate, of
             multiply(n)
         for n in range(len(units) + DRAIN_LAG + PACK_LAG):
             if n == GATE_UNITS[0] + 1:
-                prepare_weight(2)
+                prepare_weight(2, 0)
                 gather_gates("w_raw2")
             if n < len(units):
                 activate(n)

@@ -194,16 +194,16 @@ def tile_picked_zsmoe_gelu_po_kernel(tc, x_words, x_scales, w1, w2, w3, gate, of
                 nc.vector.tensor_scalar(gated[i, d][:], act, factor, None, MULT)
 
         def turn(i):
-            first_layer = 1 if i >= VECTOR_SUM_FROM else 0
-            for d in range(first_layer, D):
+            layers = (1, 2) if i == TILES - 1 else (2, 1) if i >= VECTOR_SUM_FROM else (0, 2, 1)
+            for d in layers:
                 for t in range(PACK):
                     nc.tensor.matmul(
                         turn_banks[i % TURN_BANKS][:, t, :],
                         gated[i, d][:, t * P:(t + 1) * P],
                         ident[:],
                         is_transpose=True,
-                        start=(d == first_layer and t == 0),
-                        stop=(d == D - 1 and t == PACK - 1),
+                        start=(d == layers[0] and t == 0),
+                        stop=(d == layers[-1] and t == PACK - 1),
                     )
 
         def drain(i):

@@ -36,7 +36,7 @@ PRODUCT_BANKS = 4
 TURN_BANKS = BANKS - PRODUCT_BANKS
 GATE_UNITS = (3, 12)
 STAGGER = 4
-VECTOR_SUM_FROM = 4
+VECTOR_SUM_FROM = 3
 DRAIN_LAG = 2
 PACK_LAG = 2
 PAIR = 2

@@ -22,21 +22,23 @@ U16 = mybir.dt.uint16
 U8 = mybir.dt.uint8
 FP8X4 = mybir.dt.float8_e4m3fn_x4
 GELU = mybir.ActivationFunctionType.Gelu_apprx_tanh
+COPY = mybir.ActivationFunctionType.Copy
 MULT = mybir.AluOpType.mult
 ADD = mybir.AluOpType.add
 
 HALF = N // 2
-W1_SCALAR = 384
+W1_SCALAR = 128
+W1_FIRST_ROWS = 1
 W2_SCALAR = 128
-GATE_ROWS = slice(4, 4 * (D + 1), 4)
-WORD_PIECES = ((0, 256), (256, 256), (512, 512))
+GATE_ROW = P - D
+WORD_PIECES = ((0, 128), (128, 128), (256, 256), (512, 512))
 GATE_TILES = 4
 BANKS = 8
 PRODUCT_BANKS = 4
 TURN_BANKS = BANKS - PRODUCT_BANKS
-GATE_UNITS = (3, 12)
-STAGGER = 4
-VECTOR_SUM_FROM = 3
+BLOCK = 4
+VECTOR_SUM_FROM = 4
+VECTOR_DRAINS = (4,)
 DRAIN_LAG = 2
 PACK_LAG = 2
 PAIR = 2
@@ -65,29 +67,49 @@ def tile_picked_zsmoe_gelu_po_kernel(tc, x_words, x_scales, w1, w2, w3, gate, of
 
         nc.vector.memset(scale_window[:].bitcast(I32), 0)
         nc.vector.memset(warm[:, 0:1], 0.0)
-        nc.vector.memset(gate_window[:], 0.0)
+        nc.vector.memset(gate_window[:GATE_ROW, :], 0.0)
         make_identity(nc, ident[:])
 
         w_rows = [w.rearrange("(p t) m -> p t m", t=PACK) for w in (w1, w2, w3)]
         w_raw = [keep.tile([P, PACK, N], F32, name=f"w_raw{d}", align_bytes=64) for d in range(D)]
         w2_head = keep.tile([P, PACK, W2_SCALAR], F32, name="w2_head", align_bytes=64)
 
-        nc.sync.dma_start(w_raw[0][:, :1, :], w_rows[0][:, :1, :])
+        nc.scalar.dma_start(gate_window[GATE_ROW:, :], gate[:, 0, :])
         nc.sync.dma_start(offsets[:], offs)
+        nc.sync.dma_start(w_raw[0][:, :W1_FIRST_ROWS, :], w_rows[0][:, :W1_FIRST_ROWS, :])
         for r in range(SCALE_ROWS):
             nc.sync.dma_start(
                 scale_window[r:P:QUADRANT, :].bitcast(I32), x_scales[0, r:K // 32:SCALE_ROWS, :].bitcast(I32)
             )
-        nc.sync.dma_start(w_raw[0][:, 1:, :], w_rows[0][:, 1:, :])
+        nc.sync.dma_start(w_raw[0][:, W1_FIRST_ROWS:, :], w_rows[0][:, W1_FIRST_ROWS:, :])
         nc.sync.dma_start(word_window[:].bitcast(I32), x_words[0].rearrange("p n t -> p (n t)").bitcast(I32))
         nc.sync.dma_start(w2_head[:], w_rows[1][:, :, :W2_SCALAR])
-        nc.sync.dma_start(gate_window[GATE_ROWS, :], gate[:, 0, :])
         nc.sync.dma_start(w_raw[1][:, :, W2_SCALAR:], w_rows[1][:, :, W2_SCALAR:])
         nc.sync.dma_start(w_raw[2][:], w_rows[2])
 
         nc.scalar.activation(warm[:, 1:2], warm[:, 0:1], GELU)
 
-        w_bf = [keep.tile([P, PACK * N], BF16, name=f"w_bf{d}", align_bytes=64) for d in range(D - 1)]
+        def entries(first, count):
+            return offsets[:, first // LIST_ROWS:(first + count) // LIST_ROWS]
+
+        banks = [psum.tile([P, N], F32, name=f"bank{b}") for b in range(BANKS)]
+        turn_banks = [bank[:].rearrange("p (t j) -> p t j", t=PACK) for bank in banks[PRODUCT_BANKS:]]
+
+        gate_rows = keep.tile([P, S], F32, name="gate_rows", align_bytes=64)
+        gates = keep.tile([P, TILES, D], F32, name="gates", align_bytes=64)
+        gate_banks = turn_banks[TURN_BANKS - TILES // GATE_TILES:]
+        for u, bank in enumerate(gate_banks):
+            first = u * GATE_TILES * P
+            nc.scalar.activation(
+                gate_rows[:, first:first + GATE_TILES * P], gate_window[:].indirect(entries(first, GATE_TILES * P)), COPY
+            )
+            for a in range(GATE_TILES):
+                nc.tensor.transpose(bank[:, a, :], gate_rows[:, first + a * P:first + (a + 1) * P], ident[:])
+
+        token_scales = keep.tile([P, S], U8, name="token_scales", align_bytes=64)
+        nc.vector.tensor_copy(token_scales[:], scale_window[:].indirect(offsets[:]))
+
+        w_bf = [keep.tile([P, PACK * N], BF16, name=f"w_bf{d}", align_bytes=64) for d in range(D)]
         w_codes = [keep.tile([P, N], U32, name=f"w_codes{d}", align_bytes=64) for d in range(D)]
         w_scales = [keep.tile([P, N], U8, name=f"w_scales{d}", align_bytes=64) for d in range(D)]
 
@@ -107,71 +129,34 @@ def tile_picked_zsmoe_gelu_po_kernel(tc, x_words, x_scales, w1, w2, w3, gate, of
             for first in (0, HALF):
                 quantize_weight(d, first)
 
-        def entries(first, count):
-            return offsets[:, first // LIST_ROWS:(first + count) // LIST_ROWS]
-
-        round_weight(nc.scalar.copy, 0, 0, HALF)
-        round_weight(nc.scalar.copy, 0, HALF, W1_SCALAR)
+        round_weight(nc.scalar.copy, 0, 0, W1_SCALAR)
+        round_weight(nc.vector.tensor_copy, 0, HALF, N)
+        round_weight(nc.vector.tensor_copy, 0, W1_SCALAR, HALF)
+        for u, bank in enumerate(gate_banks):
+            quantize_weight(0, HALF - u * HALF)
+            nc.vector.tensor_copy(gates[:, u * GATE_TILES:(u + 1) * GATE_TILES, :], bank[:, :, GATE_ROW:])
         interleave(nc.scalar.copy, w_bf[1][:, :PACK * W2_SCALAR], w2_head[:])
 
-        token_scales = keep.tile([P, S], U8, name="token_scales", align_bytes=64)
-        nc.vector.tensor_copy(token_scales[:], scale_window[:].indirect(offsets[:]))
         token_words = keep.tile([P, S], U32, name="token_words", align_bytes=64)
-
-        def gather_words(first, count):
+        for first, count in WORD_PIECES:
             nc.vector.tensor_copy(token_words[:, first:first + count], word_window[:].indirect(entries(first, count)))
-
-        quantize_weight(0, 0)
-        gather_words(*WORD_PIECES[0])
-        round_weight(nc.vector.tensor_copy, 0, W1_SCALAR, N)
-        quantize_weight(0, HALF)
-        for piece in WORD_PIECES[1:]:
-            gather_words(*piece)
-
-        banks = [psum.tile([P, N], F32, name=f"bank{b}") for b in range(BANKS)]
-        turn_banks = [bank[:].rearrange("p (t j) -> p t j", t=PACK) for bank in banks[PRODUCT_BANKS:]]
-        gate_rows = []
-        gates = []
-
-        def gather_gates(tag):
-            u = len(gate_rows)
-            gate_rows.append(keep.tile([P, GATE_TILES * P], F32, name=f"gate_rows{u}", tag=tag, align_bytes=64))
-            nc.vector.tensor_copy(gate_rows[u][:], gate_window[:].indirect(entries(u * GATE_TILES * P, GATE_TILES * P)))
-
-        def gate_bank(u):
-            return BANKS - len(GATE_UNITS) + u
-
-        def turn_gates(u, tag):
-            bank = turn_banks[gate_bank(u) - PRODUCT_BANKS]
-            for a in range(GATE_TILES):
-                nc.tensor.transpose(bank[:, a, :], gate_rows[u][:, a * P:(a + 1) * P], ident[:])
-            gates.append(keep.tile([P, GATE_TILES, D], F32, name=f"gates{u}", tag=tag, align_bytes=64))
-            nc.vector.tensor_copy(gates[u][:], bank[:, :, GATE_ROWS])
-
-        gather_gates("gate_rows0")
         prepare_weight(1, W2_SCALAR)
-        w_bf.append(keep.tile([P, PACK * N], BF16, name="w_bf2", tag="w_bf1", align_bytes=64))
 
         y_codes = keep.tile([P, S], U32, name="y_codes", align_bytes=64)
         y_scales = keep.tile([P, S], U8, name="y_scales", align_bytes=64)
         out_rows = out_0.rearrange("(p t) j -> p t j", t=PACK)
         out_words = out_1[0].rearrange("p n t -> p (n t)").bitcast(I32)
 
-        units = [(i, 0) for i in range(TILES)]
-        for j in range(TILES + STAGGER):
-            units.extend(unit for unit in ((j, 1), (j - STAGGER, 2)) if 0 <= unit[0] < TILES)
-        rotating = [n for n in range(len(units)) if n not in GATE_UNITS]
+        units = [(i, 0) for i in range(TILES)] + [(i, d) for d in (1, 2) for i in range(BLOCK)]
+        units += [(i, d) for i in range(BLOCK, TILES) for d in (1, 2)]
         acts = {}
         gated = {}
         ys = [keep.tile([P, PACK, PAIR * P], F32, name=f"y{pair}") for pair in range(TILES // PAIR)]
 
-        def product_bank(n):
-            return banks[gate_bank(GATE_UNITS.index(n)) if n in GATE_UNITS else rotating.index(n) % PRODUCT_BANKS]
-
         def multiply(n):
             i, d = units[n]
             nc.tensor.matmul_mx(
-                out=product_bank(n)[:],
+                out=banks[n % PRODUCT_BANKS][:],
                 lhsT=token_words[:, i * P:(i + 1) * P].bitcast(FP8X4),
                 lhsT_scale=token_scales[:, i * P:(i + 1) * P],
                 rhs=w_codes[d][:].bitcast(FP8X4),
@@ -182,33 +167,33 @@ def tile_picked_zsmoe_gelu_po_kernel(tc, x_words, x_scales, w1, w2, w3, gate, of
 
         def activate(n):
             acts[units[n]] = keep.tile([P, PACK, P], F32, name=f"act{n}")
-            nc.scalar.activation(acts[units[n]][:], product_bank(n)[:].rearrange("p (m t) -> p t m", t=PACK), GELU)
+            nc.scalar.activation(
+                acts[units[n]][:], banks[n % PRODUCT_BANKS][:].rearrange("p (m t) -> p t m", t=PACK), GELU
+            )
 
         def weigh(i, d):
             gated[i, d] = keep.tile([P, PACK * P], F32, name=f"gated{i}{d}")
             act = acts[i, d][:].rearrange("p t m -> p (t m)")
-            factor = gates[i // GATE_TILES][:, i % GATE_TILES, d:d + 1]
             if d == 1 and i >= VECTOR_SUM_FROM:
-                nc.vector.scalar_tensor_tensor(gated[i, d][:], act, factor, gated[i, 0][:], MULT, ADD)
+                nc.vector.scalar_tensor_tensor(gated[i, d][:], act, gates[:, i, d:d + 1], gated[i, 0][:], MULT, ADD)
             else:
-                nc.vector.tensor_scalar(gated[i, d][:], act, factor, None, MULT)
+                nc.vector.tensor_scalar(gated[i, d][:], act, gates[:, i, d:d + 1], None, MULT)
 
-        def turn(i):
-            layers = (1, 2) if i == TILES - 1 else (2, 1) if i >= VECTOR_SUM_FROM else (0, 2, 1)
-            for d in layers:
-                for t in range(PACK):
-                    nc.tensor.matmul(
-                        turn_banks[i % TURN_BANKS][:, t, :],
-                        gated[i, d][:, t * P:(t + 1) * P],
-                        ident[:],
-                        is_transpose=True,
-                        start=(d == layers[0] and t == 0),
-                        stop=(d == layers[-1] and t == PACK - 1),
-                    )
+        def turn(i, d, opens, closes):
+            for t in range(PACK):
+                nc.tensor.matmul(
+                    turn_banks[i % TURN_BANKS][:, t, :],
+                    gated[i, d][:, t * P:(t + 1) * P],
+                    ident[:],
+                    is_transpose=True,
+                    start=(opens and t == 0),
+                    stop=(closes and t == PACK - 1),
+                )
 
         def drain(i):
             pair, place = divmod(i, PAIR)
-            nc.scalar.copy(ys[pair][:, :, place * P:(place + 1) * P], turn_banks[i % TURN_BANKS])
+            copy = nc.vector.tensor_copy if i in VECTOR_DRAINS else nc.scalar.copy
+            copy(ys[pair][:, :, place * P:(place + 1) * P], turn_banks[i % TURN_BANKS])
             if place == PAIR - 1:
                 nc.sync.dma_start(out_rows[:, :, pair * PAIR * P:(i + 1) * P], ys[pair][:])
 
@@ -217,37 +202,41 @@ def tile_picked_zsmoe_gelu_po_kernel(tc, x_words, x_scales, w1, w2, w3, gate, of
             pair, place = divmod(group[0], PAIR)
             y = ys[pair][:, :, place * P:(place + len(group)) * P]
             y_bf = keep.tile([P, PACK * P * len(group)], BF16, name=f"y_bf{group[0]}", align_bytes=64)
-            interleave(nc.scalar.copy if group == GROUPS[-1] else nc.vector.tensor_copy, y_bf[:], y)
+            interleave(nc.vector.tensor_copy, y_bf[:], y)
             nc.vector.quantize_mx(out=y_codes[:, cols].bitcast(FP8X4), scales=y_scales[:, cols], in_=y_bf[:])
             if group[-1] % PAIR == PAIR - 1:
                 pair_cols = slice(pair * PAIR * P, cols.stop)
                 nc.sync.dma_start(out_words[:, pair_cols], y_codes[:, pair_cols].bitcast(I32))
 
-        weighed, packed = set(), set()
-        turned, drained = {}, {}
+        turned, drained, packed = {}, {}, set()
         for n in range(PRODUCT_BANKS):
             multiply(n)
         for n in range(len(units) + DRAIN_LAG + PACK_LAG):
-            if n == GATE_UNITS[0] + 1:
-                prepare_weight(2, 0)
-                gather_gates("w_raw2")
             if n < len(units):
                 activate(n)
             if n + PRODUCT_BANKS < len(units):
                 multiply(n + PRODUCT_BANKS)
-            if n in GATE_UNITS:
-                turn_gates(GATE_UNITS.index(n), ("w_raw1", "gates1")[GATE_UNITS.index(n)])
-            for i in turned:
-                if i not in drained and n >= turned[i] + DRAIN_LAG:
-                    drain(i)
-                    drained[i] = n
-            for i, d in units[:n + 1]:
-                if (i, d) not in weighed and i // GATE_TILES < len(gates) and (i < TURN_BANKS or i - TURN_BANKS in drained):
+            for i in [i for i in turned if i not in drained and n >= turned[i] + DRAIN_LAG][:1]:
+                drain(i)
+                drained[i] = n
+            if n < len(units):
+                i, d = units[n]
+                early = i < VECTOR_SUM_FROM
+                if d == 0 and early:
                     weigh(i, d)
-                    weighed.add((i, d))
-                    if d == D - 1:
-                        turn(i)
-                        turned[i] = n
+                    turn(i, d, True, False)
+                elif d == 1:
+                    if not early:
+                        weigh(i, 0)
+                    weigh(i, 1)
+                elif d == 2:
+                    weigh(i, 2)
+                    layers = (1, 2) if i == TILES - 1 else (2, 1)
+                    turn(i, layers[0], not early, False)
+                    turn(i, layers[1], False, True)
+                    turned[i] = n
+            if n == VECTOR_SUM_FROM - 1:
+                prepare_weight(2, 0)
             for group in GROUPS:
                 if group not in packed and group[-1] in drained and n >= drained[group[-1]] + PACK_LAG:
                     pack(group)

@@ -38,6 +38,7 @@ PRODUCT_BANKS = 4
 TURN_BANKS = BANKS - PRODUCT_BANKS
 BLOCK = 4
 VECTOR_SUM_FROM = 4
+VECTOR_SUM_TO = 4
 VECTOR_DRAINS = (4,)
 DRAIN_LAG = 2
 PACK_LAG = 2
@@ -174,8 +175,8 @@ def tile_picked_zsmoe_gelu_po_kernel(tc, x_words, x_scales, w1, w2, w3, gate, of
         def weigh(i, d):
             gated[i, d] = keep.tile([P, PACK * P], F32, name=f"gated{i}{d}")
             act = acts[i, d][:].rearrange("p t m -> p (t m)")
-            if d == 1 and i >= VECTOR_SUM_FROM:
-                nc.vector.scalar_tensor_tensor(gated[i, d][:], act, gates[:, i, d:d + 1], gated[i, 0][:], MULT, ADD)
+            if (d == 1 and i >= VECTOR_SUM_FROM) or (d == 2 and i < VECTOR_SUM_TO):
+                nc.vector.scalar_tensor_tensor(gated[i, d][:], act, gates[:, i, d:d + 1], gated[i, d - 1][:], MULT, ADD)
             else:
                 nc.vector.tensor_scalar(gated[i, d][:], act, gates[:, i, d:d + 1], None, MULT)
 
@@ -231,9 +232,9 @@ def tile_picked_zsmoe_gelu_po_kernel(tc, x_words, x_scales, w1, w2, w3, gate, of
                     weigh(i, 1)
                 elif d == 2:
                     weigh(i, 2)
-                    layers = (1, 2) if i == TILES - 1 else (2, 1)
-                    turn(i, layers[0], not early, False)
-                    turn(i, layers[1], False, True)
+                    layers = (2,) if i < VECTOR_SUM_TO else (1, 2) if i == TILES - 1 else (2, 1)
+                    for layer in layers:
+                        turn(i, layer, layer == layers[0] and not early, layer == layers[-1])
                     turned[i] = n
             if n == VECTOR_SUM_FROM - 1:
                 prepare_weight(2, 0)

from contextlib import ExitStack

import concourse.mybir as mybir
from concourse.masks import make_identity

K, T, S, D, N = 512, 2048, 1024, 3, 512
P = 128
PACK = 4
QUADRANT = 32
SCALE_ROWS = 4
LIST_ROWS = 16
TILES = S // P

FLOPS = 2 * D * K * N * S
BYTES = K * T + K // 32 * T + 4 * D * K * N + 4 * D * T + 2 * P * S // LIST_ROWS + 4 * N * S + N * S + N // 32 * S

F32 = mybir.dt.float32
BF16 = mybir.dt.bfloat16
I32 = mybir.dt.int32
U32 = mybir.dt.uint32
U16 = mybir.dt.uint16
U8 = mybir.dt.uint8
FP8X4 = mybir.dt.float8_e4m3fn_x4
GELU = mybir.ActivationFunctionType.Gelu_apprx_tanh
COPY = mybir.ActivationFunctionType.Copy
MULT = mybir.AluOpType.mult
ADD = mybir.AluOpType.add

HALF = N // 2
W1_SCALAR = 128
W1_FIRST_ROWS = 1
W2_SCALAR = 128
GATE_ROW = P - D
WORD_PIECES = ((0, 128), (128, 128), (256, 256), (512, 512))
GATE_TILES = 4
BANKS = 8
PRODUCT_BANKS = 4
TURN_BANKS = BANKS - PRODUCT_BANKS
BLOCK = 4
VECTOR_SUM_FROM = 4
VECTOR_SUM_TO = 4
VECTOR_DRAINS = (4,)
DRAIN_LAG = 2
PACK_LAG = 2
PAIR = 2
GROUPS = ((0, 1), (2, 3), (4, 5), (6,), (7,))


def interleave(copy, dst, src):
    copy(
        out=dst.rearrange("p (c i t) -> p c t i", i=4, t=PACK),
        in_=src.rearrange("p t (c i) -> p c t i", i=4),
    )


def tile_picked_zsmoe_gelu_po_kernel(tc, x_words, x_scales, w1, w2, w3, gate, offs, out_0, out_1, out_2):
    nc = tc.nc
    with ExitStack() as ctx:
        keep = ctx.enter_context(tc.tile_pool(name="keep", bufs=1))
        psum = ctx.enter_context(tc.psum_pool(name="psum", bufs=1))

        offsets = keep.tile([P, S // LIST_ROWS], U16, name="offsets")
        word_window = keep.tile([P, T], U32, name="word_window", align_bytes=64)
        scale_window = keep.tile([P, T], U8, name="scale_window", align_bytes=64)
        gate_window = keep.tile([P, T], F32, name="gate_window", align_bytes=64)
        ident = keep.tile([P, P], F32, name="ident", align_bytes=64)
        warm = keep.tile([P, 2], F32, name="warm")

        nc.vector.memset(scale_window[:].bitcast(I32), 0)
        nc.vector.memset(warm[:, 0:1], 0.0)
        nc.vector.memset(gate_window[:GATE_ROW, :], 0.0)
        make_identity(nc, ident[:])

        w_rows = [w.rearrange("(p t) m -> p t m", t=PACK) for w in (w1, w2, w3)]
        w_raw = [keep.tile([P, PACK, N], F32, name=f"w_raw{d}", align_bytes=64) for d in range(D)]
        w2_head = keep.tile([P, PACK, W2_SCALAR], F32, name="w2_head", align_bytes=64)

        nc.scalar.dma_start(gate_window[GATE_ROW:, :], gate[:, 0, :])
        nc.sync.dma_start(offsets[:], offs)
        nc.sync.dma_start(w_raw[0][:, :W1_FIRST_ROWS, :], w_rows[0][:, :W1_FIRST_ROWS, :])
        for r in range(SCALE_ROWS):
            nc.sync.dma_start(
                scale_window[r:P:QUADRANT, :].bitcast(I32), x_scales[0, r:K // 32:SCALE_ROWS, :].bitcast(I32)
            )
        nc.sync.dma_start(w_raw[0][:, W1_FIRST_ROWS:, :], w_rows[0][:, W1_FIRST_ROWS:, :])
        nc.sync.dma_start(word_window[:].bitcast(I32), x_words[0].rearrange("p n t -> p (n t)").bitcast(I32))
        nc.sync.dma_start(w2_head[:], w_rows[1][:, :, :W2_SCALAR])
        nc.sync.dma_start(w_raw[1][:, :, W2_SCALAR:], w_rows[1][:, :, W2_SCALAR:])
        nc.sync.dma_start(w_raw[2][:], w_rows[2])

        nc.scalar.activation(warm[:, 1:2], warm[:, 0:1], GELU)

        def entries(first, count):
            return offsets[:, first // LIST_ROWS:(first + count) // LIST_ROWS]

        banks = [psum.tile([P, N], F32, name=f"bank{b}") for b in range(BANKS)]
        turn_banks = [bank[:].rearrange("p (t j) -> p t j", t=PACK) for bank in banks[PRODUCT_BANKS:]]

        gate_rows = keep.tile([P, S], F32, name="gate_rows", align_bytes=64)
        gates = keep.tile([P, TILES, D], F32, name="gates", align_bytes=64)
        gate_banks = turn_banks[TURN_BANKS - TILES // GATE_TILES:]
        for u, bank in enumerate(gate_banks):
            first = u * GATE_TILES * P
            nc.scalar.activation(
                gate_rows[:, first:first + GATE_TILES * P], gate_window[:].indirect(entries(first, GATE_TILES * P)), COPY
            )
            for a in range(GATE_TILES):
                nc.tensor.transpose(bank[:, a, :], gate_rows[:, first + a * P:first + (a + 1) * P], ident[:])

        token_scales = keep.tile([P, S], U8, name="token_scales", align_bytes=64)
        nc.vector.tensor_copy(token_scales[:], scale_window[:].indirect(offsets[:]))

        w_bf = [keep.tile([P, PACK * N], BF16, name=f"w_bf{d}", align_bytes=64) for d in range(D)]
        w_codes = [keep.tile([P, N], U32, name=f"w_codes{d}", align_bytes=64) for d in range(D)]
        w_scales = [keep.tile([P, N], U8, name=f"w_scales{d}", align_bytes=64) for d in range(D)]

        def round_weight(copy, d, first, last):
            interleave(copy, w_bf[d][:, PACK * first:PACK * last], w_raw[d][:, :, first:last])

        def quantize_weight(d, first):
            nc.vector.quantize_mx(
                out=w_codes[d][:, first:first + HALF].bitcast(FP8X4),
                scales=w_scales[d][:, first:first + HALF],
                in_=w_bf[d][:, PACK * first:PACK * (first + HALF)],
            )

        def prepare_weight(d, rounded):
            round_weight(nc.vector.tensor_copy, d, rounded, HALF)
            round_weight(nc.vector.tensor_copy, d, HALF, N)
            for first in (0, HALF):
                quantize_weight(d, first)

        round_weight(nc.scalar.copy, 0, 0, W1_SCALAR)
        round_weight(nc.vector.tensor_copy, 0, HALF, N)
        round_weight(nc.vector.tensor_copy, 0, W1_SCALAR, HALF)
        for u, bank in enumerate(gate_banks):
            quantize_weight(0, HALF - u * HALF)
            nc.vector.tensor_copy(gates[:, u * GATE_TILES:(u + 1) * GATE_TILES, :], bank[:, :, GATE_ROW:])
        interleave(nc.scalar.copy, w_bf[1][:, :PACK * W2_SCALAR], w2_head[:])

        token_words = keep.tile([P, S], U32, name="token_words", align_bytes=64)
        for first, count in WORD_PIECES:
            nc.vector.tensor_copy(token_words[:, first:first + count], word_window[:].indirect(entries(first, count)))
        prepare_weight(1, W2_SCALAR)

        y_codes = keep.tile([P, S], U32, name="y_codes", align_bytes=64)
        y_scales = keep.tile([P, S], U8, name="y_scales", align_bytes=64)
        out_rows = out_0.rearrange("(p t) j -> p t j", t=PACK)
        out_words = out_1[0].rearrange("p n t -> p (n t)").bitcast(I32)

        units = [(i, 0) for i in range(TILES)] + [(i, d) for d in (1, 2) for i in range(BLOCK)]
        units += [(i, d) for i in range(BLOCK, TILES) for d in (1, 2)]
        acts = {}
        gated = {}
        ys = [keep.tile([P, PACK, PAIR * P], F32, name=f"y{pair}") for pair in range(TILES // PAIR)]

        def multiply(n):
            i, d = units[n]
            nc.tensor.matmul_mx(
                out=banks[n % PRODUCT_BANKS][:],
                lhsT=token_words[:, i * P:(i + 1) * P].bitcast(FP8X4),
                lhsT_scale=token_scales[:, i * P:(i + 1) * P],
                rhs=w_codes[d][:].bitcast(FP8X4),
                rhs_scale=w_scales[d][:],
                start=True,
                stop=True,
            )

        def activate(n):
            acts[units[n]] = keep.tile([P, PACK, P], F32, name=f"act{n}")
            nc.scalar.activation(
                acts[units[n]][:], banks[n % PRODUCT_BANKS][:].rearrange("p (m t) -> p t m", t=PACK), GELU
            )

        def weigh(i, d):
            gated[i, d] = keep.tile([P, PACK * P], F32, name=f"gated{i}{d}")
            act = acts[i, d][:].rearrange("p t m -> p (t m)")
            if (d == 1 and i >= VECTOR_SUM_FROM) or (d == 2 and i < VECTOR_SUM_TO):
                nc.vector.scalar_tensor_tensor(gated[i, d][:], act, gates[:, i, d:d + 1], gated[i, d - 1][:], MULT, ADD)
            else:
                nc.vector.tensor_scalar(gated[i, d][:], act, gates[:, i, d:d + 1], None, MULT)

        def turn(i, d, opens, closes):
            for t in range(PACK):
                nc.tensor.matmul(
                    turn_banks[i % TURN_BANKS][:, t, :],
                    gated[i, d][:, t * P:(t + 1) * P],
                    ident[:],
                    is_transpose=True,
                    start=(opens and t == 0),
                    stop=(closes and t == PACK - 1),
                )

        def drain(i):
            pair, place = divmod(i, PAIR)
            copy = nc.vector.tensor_copy if i in VECTOR_DRAINS else nc.scalar.copy
            copy(ys[pair][:, :, place * P:(place + 1) * P], turn_banks[i % TURN_BANKS])
            if place == PAIR - 1:
                nc.sync.dma_start(out_rows[:, :, pair * PAIR * P:(i + 1) * P], ys[pair][:])

        def pack(group):
            cols = slice(group[0] * P, (group[-1] + 1) * P)
            pair, place = divmod(group[0], PAIR)
            y = ys[pair][:, :, place * P:(place + len(group)) * P]
            y_bf = keep.tile([P, PACK * P * len(group)], BF16, name=f"y_bf{group[0]}", align_bytes=64)
            interleave(nc.vector.tensor_copy, y_bf[:], y)
            nc.vector.quantize_mx(out=y_codes[:, cols].bitcast(FP8X4), scales=y_scales[:, cols], in_=y_bf[:])
            if group[-1] % PAIR == PAIR - 1:
                pair_cols = slice(pair * PAIR * P, cols.stop)
                nc.sync.dma_start(out_words[:, pair_cols], y_codes[:, pair_cols].bitcast(I32))

        turned, drained, packed = {}, {}, set()
        for n in range(PRODUCT_BANKS):
            multiply(n)
        for n in range(len(units) + DRAIN_LAG + PACK_LAG):
            if n < len(units):
                activate(n)
            if n + PRODUCT_BANKS < len(units):
                multiply(n + PRODUCT_BANKS)
            for i in [i for i in turned if i not in drained and n >= turned[i] + DRAIN_LAG][:1]:
                drain(i)
                drained[i] = n
            if n < len(units):
                i, d = units[n]
                early = i < VECTOR_SUM_FROM
                if d == 0 and early:
                    weigh(i, d)
                    turn(i, d, True, False)
                elif d == 1:
                    if not early:
                        weigh(i, 0)
                    weigh(i, 1)
                elif d == 2:
                    weigh(i, 2)
                    layers = (2,) if i < VECTOR_SUM_TO else (1, 2) if i == TILES - 1 else (2, 1)
                    for layer in layers:
                        turn(i, layer, layer == layers[0] and not early, layer == layers[-1])
                    turned[i] = n
            if n == VECTOR_SUM_FROM - 1:
                prepare_weight(2, 0)
            for group in GROUPS:
                if group not in packed and group[-1] in drained and n >= drained[group[-1]] + PACK_LAG:
                    pack(group)
                    packed.add(group)

        for r in range(SCALE_ROWS):
            queue = (nc.sync, nc.scalar)[r % 2]
            queue.dma_start(
                out_2[0, r:N // 32:SCALE_ROWS, :].bitcast(I32), y_scales[r:P:QUADRANT, :].bitcast(I32)
            )
